import numpy as np
import ml_dtypes


def mxq(x, axis, fmt="e4m3"):
    dtype, down = {"e4m3": (ml_dtypes.float8_e4m3fn, 7), "e5m2": (ml_dtypes.float8_e5m2, 14)}[fmt]
    v = np.moveaxis(np.asarray(x, np.float32).astype(ml_dtypes.bfloat16).astype(np.float64), axis, -1)
    blocks = v.reshape(v.shape[:-1] + (-1, 32))
    amax = np.abs(blocks).max(-1, keepdims=True)
    byte = np.maximum(np.where(amax > 0, np.frexp(amax)[1] - 1 + 127, 0) - down, 1)
    scale = np.exp2(byte - 127.0)
    codes = (blocks / scale).astype(np.float32).astype(dtype).astype(np.float64)
    return np.moveaxis((codes * scale).reshape(v.shape), -1, axis)


WIDE = False


def mx_kscale(k):
    if not WIDE:
        return np.ones(k)
    levels = np.array([30, -30])
    if k % 512:
        return np.exp2(np.random.permutation(np.resize(levels, k // 32))).repeat(32)
    a = np.empty((k // 512, 16))
    for p in range(k // 512):
        a[p, :8] = np.random.permutation(np.resize(levels, 8))
        for g in range(8):
            far = levels[np.abs(levels - a[p, g]) >= 10]
            a[p, g + 8] = far[np.random.randint(len(far))]
    return np.exp2(a.ravel()).repeat(32)


def f64(x):
    return np.asarray(x).astype(np.float64)


def striped(idx):
    return np.tile(idx.reshape(-1, 16).T, (8, 1)).astype(np.uint16)


def unstriped(offs):
    return offs[:16].T.reshape(-1).astype(np.int64)


def planes(y):
    n, m = y.shape
    v = y.astype(np.float32).astype(ml_dtypes.bfloat16).astype(np.float64).reshape(n // 32, 32, m)
    top = np.abs(v).max(1)
    byte = np.clip(np.where(top > 0, np.frexp(top)[1] - 1 + 127 - 7, 1), 1, 254)
    codes = (v * np.exp2(127.0 - byte)[:, None, :]).reshape(n, m).astype(np.float32).astype(ml_dtypes.float8_e4m3fn).view(np.uint8)
    words = codes.reshape(n // 512, 128, 4, m).transpose(0, 1, 3, 2)
    return np.ascontiguousarray(words), np.ascontiguousarray(byte.astype(np.uint8).reshape(n // 512, 16, m))


def split(x):
    m, e = np.frexp(f64(x))
    hi = np.ldexp(np.trunc(16.0 * m) / 16.0, e)
    return hi, f64(x) - hi


K, N, T, J = 512, 512, 2048, 1024


def setup_inputs():
    n = np.random.standard_normal
    s = mx_kscale(K)[:, None]
    m = np.exp(0.5 * n((1, J)))
    return {
        "dy": (m * n((K, J)) * s).astype(np.float32),
        "w": (n((K, N)) / np.sqrt(K) / s).astype(np.float32),
        "wgo": np.tile(np.random.uniform(0.5, 2.0, J), (128, 1)).astype(np.float32),
        "offs": striped(np.random.permutation(T)[:J]),
    }


def reference(dy, w, wgo, offs):
    idx = unstriped(offs)
    dy_ = mxq(f64(dy), 0, "e5m2")
    w_hi, w_lo = split(w)
    w_hi_, w_lo_ = mxq(w_hi, 0, "e4m3"), mxq(w_lo, 0, "e4m3")
    dx = w_hi_.T @ dy_ + w_lo_.T @ dy_
    out = np.zeros((N, T))
    out[:, idx] = f64(wgo)[0] * (dx)
    return (out,) + planes(out)

@@ -1,0 +1,216 @@
+from contextlib import ExitStack
+
+import concourse.mybir as mybir
+
+K, N, T, J = 512, 512, 2048, 1024
+FLOPS = 2 * 2 * K * N * J
+
+F32 = mybir.dt.float32
+BF16 = mybir.dt.bfloat16
+I32 = mybir.dt.int32
+U32 = mybir.dt.uint32
+U16 = mybir.dt.uint16
+U8 = mybir.dt.uint8
+E4M3 = mybir.dt.float8_e4m3fn_x4
+E5M2 = mybir.dt.float8_e5m2_x4
+ALU = mybir.AluOpType
+
+P = 128
+PACK = 4
+HALF = 512
+PIECE = 256
+HI_MASK = -(1 << 20)
+CHUNK = 256
+CHUNKS = T // CHUNK
+VECTOR_CHUNKS = 5
+
+
+def tile_list_embg_hl_noneP_kernel(tc, dy, w, wgo, offs, out_0, out_1, out_2):
+    nc = tc.nc
+    with ExitStack() as ctx:
+        keep = ctx.enter_context(tc.tile_pool(name="keep", bufs=1))
+        psum = ctx.enter_context(tc.psum_pool(name="psum", bufs=1))
+
+        w_rows = w.rearrange("(p i) n -> p i n", i=PACK)
+        dy_rows = dy.rearrange("(p i) j -> p i j", i=PACK)
+        out_rows = out_0.rearrange("(p r) t -> p r t", r=PACK)
+
+        offsets = keep.tile([P, J // 16], U16, name="offsets")
+        w_raw = [keep.tile([P, PACK, PIECE], F32, name="w_raw%d" % a) for a in range(2)]
+        dy_raw = [keep.tile([P, PACK, PIECE], F32, name="dy_raw%d" % a) for a in range(4)]
+        weight = keep.tile([P, J], F32, name="weight")
+
+        for a in range(2):
+            nc.sync.dma_start(out=w_raw[a][:], in_=w_rows[:, :, a * PIECE : (a + 1) * PIECE])
+        for a in range(2):
+            nc.sync.dma_start(out=dy_raw[a][:], in_=dy_rows[:, :, a * PIECE : (a + 1) * PIECE])
+        nc.sync.dma_start(offsets[:], offs)
+        nc.sync.dma_start(out=weight[:, :HALF], in_=wgo[:, :HALF])
+        for a in range(2, 4):
+            nc.sync.dma_start(out=dy_raw[a][:], in_=dy_rows[:, :, a * PIECE : (a + 1) * PIECE])
+        nc.sync.dma_start(out=weight[:, HALF:], in_=wgo[:, HALF:])
+
+        page = [keep.tile([P, T], F32, name="page%d" % r) for r in range(2)]
+        for r in range(2):
+            nc.vector.memset(page[r][:], 0.0)
+
+        hi_bf = keep.tile([P, PACK, P, PACK], BF16, name="hi_bf", align_bytes=64)
+        lo_bf = keep.tile([P, PACK, P, PACK], BF16, name="lo_bf", tag="lo_bf", align_bytes=64)
+        for a in range(2):
+            hi = keep.tile([P, PACK, PIECE], F32, name="hi%d" % a)
+            nc.vector.tensor_scalar(
+                out=hi[:].bitcast(I32), in0=w_raw[a][:].bitcast(I32), scalar1=HI_MASK, scalar2=None, op0=ALU.bitwise_and
+            )
+            ms = slice(a * PIECE // PACK, (a + 1) * PIECE // PACK)
+            hi_src = hi[:].rearrange("p i (m r) -> p m i r", r=PACK)
+            w_src = w_raw[a][:].rearrange("p i (m r) -> p m i r", r=PACK)
+            nc.scalar.copy(out=hi_bf[:, :, ms, :].rearrange("p r m i -> p m i r"), in_=hi_src)
+            nc.vector.tensor_tensor(
+                out=lo_bf[:, :, ms, :].rearrange("p r m i -> p m i r"), in0=w_src, in1=hi_src, op=ALU.subtract
+            )
+
+        hi_codes = keep.tile([P, N], U32, name="hi_codes", align_bytes=64)
+        hi_scales = keep.tile([P, N], U8, name="hi_scales", align_bytes=64)
+        lo_codes = keep.tile([P, N], U32, name="lo_codes", align_bytes=64)
+        lo_scales = keep.tile([P, N], U8, name="lo_scales", align_bytes=64)
+
+        def quantize_w(r0, r1):
+            for src, codes, scales in ((hi_bf, hi_codes, hi_scales), (lo_bf, lo_codes, lo_scales)):
+                nc.vector.quantize_mx(
+                    out=codes[:, r0 * P : r1 * P].bitcast(E4M3),
+                    scales=scales[:, r0 * P : r1 * P],
+                    in_=src[:, r0:r1, :, :].rearrange("p r m i -> p (r m i)"),
+                )
+
+        dy_codes = [keep.tile([P, HALF], U32, name="dy_codes0", align_bytes=64)]
+        dy_scales = [keep.tile([P, HALF], U8, name="dy_scales%d" % h, align_bytes=64) for h in range(2)]
+        dy_bf = {}
+
+        def round_dy(a, copy, tag):
+            dy_bf[a] = keep.tile([P, PIECE, PACK], BF16, name="dy_bf%d" % a, tag=tag, align_bytes=64)
+            copy(
+                out=dy_bf[a][:].rearrange("p (c e) i -> p c i e", e=4),
+                in_=dy_raw[a][:].rearrange("p i (c e) -> p c i e", e=4),
+            )
+
+        def quantize_dy(a):
+            cols = slice((a % 2) * PIECE, (a % 2 + 1) * PIECE)
+            nc.vector.quantize_mx(
+                out=dy_codes[a // 2][:, cols].bitcast(E5M2),
+                scales=dy_scales[a // 2][:, cols],
+                in_=dy_bf[a][:].rearrange("p c i -> p (c i)"),
+            )
+
+        acc = {}
+
+        def product(r, h):
+            acc[r, h] = psum.tile([P, HALF], F32, name="acc%d_%d" % (r, h))
+            cols = slice(r * P, (r + 1) * P)
+            for first, codes, scales in ((True, hi_codes, hi_scales), (False, lo_codes, lo_scales)):
+                nc.tensor.matmul_mx(
+                    out=acc[r, h][:],
+                    lhsT=codes[:, cols].bitcast(E4M3),
+                    lhsT_scale=scales[:, cols],
+                    rhs=dy_codes[h][:].bitcast(E5M2),
+                    rhs_scale=dy_scales[h][:],
+                    start=first,
+                    stop=not first,
+                )
+
+        def evacuate(r, j0, j1, tag):
+            dx = keep.tile([P, j1 - j0], F32, name="dx%d_%d" % (r, j0), tag=tag, align_bytes=64)
+            for h in range(2):
+                a, b = max(j0, h * HALF), min(j1, (h + 1) * HALF)
+                if a < b:
+                    nc.scalar.copy(out=dx[:, a - j0 : b - j0], in_=acc[r, h][:, a - h * HALF : b - h * HALF])
+            return dx
+
+        def scatter(r, j0, j1, dx):
+            nc.vector.tensor_tensor(
+                page[r][:].indirect(offsets[:, j0 // 16 : j1 // 16]), dx[:], weight[:, j0:j1], ALU.mult
+            )
+
+        y_bf = keep.tile([P, T, PACK], BF16, name="y_bf", align_bytes=64)
+
+        round_dy(0, nc.scalar.copy, "dy_bf0")
+        quantize_dy(0)
+        round_dy(1, nc.vector.tensor_copy, "dy_bf1")
+        quantize_w(0, 1)
+        quantize_dy(1)
+        product(0, 0)
+        dx_first = evacuate(0, 0, HALF, "first")
+        quantize_w(1, 2)
+        quantize_w(2, 4)
+        round_dy(2, nc.scalar.copy, "dy_bf1")
+        round_dy(3, nc.scalar.copy, "lo_bf")
+        for r in range(1, PACK):
+            product(r, 0)
+        scatter(0, 0, HALF, dx_first)
+        dy_codes.append(keep.tile([P, HALF], U32, name="dy_codes1", tag="first", align_bytes=64))
+        quantize_dy(2)
+        dx_fill = evacuate(1, 0, PIECE, "dy_bf1")
+        quantize_dy(3)
+        for r in range(PACK):
+            product(r, 1)
+        dx0 = evacuate(0, HALF, J, "slot2")
+        scatter(1, 0, PIECE, dx_fill)
+        dx1 = evacuate(1, PIECE, J, "slot3")
+        scatter(0, HALF, J, dx0)
+        dx2 = evacuate(2, 0, J, "dx2")
+        dx3 = evacuate(3, 0, J, "dx3")
+        nc.sync.dma_start(out=out_rows[:, 0, :], in_=page[0][:])
+        nc.scalar.copy(out=y_bf[:, :, 0], in_=page[0][:])
+        page.append(keep.tile([P, T], F32, name="page2", tag="slot2", align_bytes=64))
+        nc.gpsimd.memset(page[2][:], 0.0)
+        scatter(1, PIECE, J, dx1)
+        nc.sync.dma_start(out=out_rows[:, 1, :], in_=page[1][:])
+        nc.scalar.copy(out=y_bf[:, :, 1], in_=page[1][:])
+        page.append(keep.tile([P, T], F32, name="page3", tag="slot3", align_bytes=64))
+        nc.gpsimd.memset(page[3][:], 0.0)
+        scatter(2, 0, J, dx2)
+        nc.sync.dma_start(out=out_rows[:, 2, :], in_=page[2][:])
+        split = VECTOR_CHUNKS * CHUNK
+        nc.scalar.copy(out=y_bf[:, :split, 2:4], in_=page[2][:, :split].unsqueeze(2).to_broadcast([P, split, 2]))
+        nc.scalar.copy(out=y_bf[:, split:, 2], in_=page[2][:, split:])
+        scatter(3, 0, J, dx3)
+        nc.sync.dma_start(out=out_rows[:, 3, :], in_=page[3][:])
+
+        y_codes = keep.tile([P, T], U32, name="y_codes", align_bytes=64)
+        y_scales = keep.tile([P, T], U8, name="y_scales", align_bytes=64)
+        words = out_1[0].rearrange("p t i -> p (t i)").bitcast(I32)
+
+        def round_last(c, copy):
+            cols = slice(c * CHUNK, (c + 1) * CHUNK)
+            copy(out=y_bf[:, cols, 3], in_=page[3][:, cols])
+
+        def quantize_y(c):
+            cols = slice(c * CHUNK, (c + 1) * CHUNK)
+            nc.vector.quantize_mx(
+                out=y_codes[:, cols].bitcast(E4M3),
+                scales=y_scales[:, cols],
+                in_=y_bf[:, cols, :].rearrange("p t i -> p (t i)"),
+            )
+
+        def store_words(c0, c1):
+            cols = slice(c0 * CHUNK, c1 * CHUNK)
+            nc.sync.dma_start(out=words[:, cols], in_=y_codes[:, cols].bitcast(I32))
+
+        for c in range(VECTOR_CHUNKS, CHUNKS):
+            round_last(c, nc.scalar.copy)
+        round_last(0, nc.vector.tensor_copy)
+        for c in range(1, VECTOR_CHUNKS):
+            round_last(c, nc.vector.tensor_copy)
+            quantize_y(c - 1)
+            if c % 2 == 0:
+                store_words(c - 2, c)
+        quantize_y(5)
+        quantize_y(4)
+        quantize_y(6)
+        store_words(4, 7)
+        quantize_y(7)
+        store_words(7, 8)
+        for q in range(4):
+            queue = nc.scalar if q % 2 else nc.sync
+            queue.dma_start(
+                out=out_2[0, 4 * q : 4 * q + 4, :].bitcast(I32), in_=y_scales[32 * q : 32 * q + 4, :].bitcast(I32)
+            )

@@ -22,7 +22,7 @@ PIECE = 256
 HI_MASK = -(1 << 20)
 CHUNK = 256
 CHUNKS = T // CHUNK
-VECTOR_CHUNKS = 5
+VECTOR_CHUNKS = 4
 
 
 def tile_list_embg_hl_noneP_kernel(tc, dy, w, wgo, offs, out_0, out_1, out_2):
@@ -45,14 +45,15 @@ def tile_list_embg_hl_noneP_kernel(tc, dy, w, wgo, offs, out_0, out_1, out_2):
         for a in range(2):
             nc.sync.dma_start(out=dy_raw[a][:], in_=dy_rows[:, :, a * PIECE : (a + 1) * PIECE])
         nc.sync.dma_start(offsets[:], offs)
-        nc.sync.dma_start(out=weight[:, :HALF], in_=wgo[:, :HALF])
+        nc.sync.dma_start(out=weight[:, :PIECE], in_=wgo[:, :PIECE])
         for a in range(2, 4):
             nc.sync.dma_start(out=dy_raw[a][:], in_=dy_rows[:, :, a * PIECE : (a + 1) * PIECE])
-        nc.sync.dma_start(out=weight[:, HALF:], in_=wgo[:, HALF:])
+        nc.sync.dma_start(out=weight[:, PIECE:], in_=wgo[:, PIECE:])
 
-        page = [keep.tile([P, T], F32, name="page%d" % r) for r in range(2)]
-        for r in range(2):
+        page = [keep.tile([P, T], F32, name="page%d" % r) for r in range(4)]
+        for r in range(4):
             nc.vector.memset(page[r][:], 0.0)
+
 
         hi_bf = keep.tile([P, PACK, P, PACK], BF16, name="hi_bf", align_bytes=64)
         lo_bf = keep.tile([P, PACK, P, PACK], BF16, name="lo_bf", tag="lo_bf", align_bytes=64)
@@ -69,18 +70,20 @@ def tile_list_embg_hl_noneP_kernel(tc, dy, w, wgo, offs, out_0, out_1, out_2):
                 out=lo_bf[:, :, ms, :].rearrange("p r m i -> p m i r"), in0=w_src, in1=hi_src, op=ALU.subtract
             )
 
-        hi_codes = keep.tile([P, N], U32, name="hi_codes", align_bytes=64)
-        hi_scales = keep.tile([P, N], U8, name="hi_scales", align_bytes=64)
-        lo_codes = keep.tile([P, N], U32, name="lo_codes", align_bytes=64)
-        lo_scales = keep.tile([P, N], U8, name="lo_scales", align_bytes=64)
+        w_codes = {}
+        w_scales = keep.tile([P, 2 * N], U8, name="w_scales", align_bytes=64)
 
-        def quantize_w(r0, r1):
-            for src, codes, scales in ((hi_bf, hi_codes, hi_scales), (lo_bf, lo_codes, lo_scales)):
+        def quantize_w(r0, r1, codes, first):
+            for part, src in enumerate((hi_bf, lo_bf)):
+                at = first + part * (r1 - r0) * P
+                plane = part * N + r0 * P
                 nc.vector.quantize_mx(
-                    out=codes[:, r0 * P : r1 * P].bitcast(E4M3),
-                    scales=scales[:, r0 * P : r1 * P],
+                    out=codes[:, at : at + (r1 - r0) * P].bitcast(E4M3),
+                    scales=w_scales[:, plane : plane + (r1 - r0) * P],
                     in_=src[:, r0:r1, :, :].rearrange("p r m i -> p (r m i)"),
                 )
+                for r in range(r0, r1):
+                    w_codes[part, r] = codes[:, at + (r - r0) * P : at + (r - r0 + 1) * P]
 
         dy_codes = [keep.tile([P, HALF], U32, name="dy_codes0", align_bytes=64)]
         dy_scales = [keep.tile([P, HALF], U8, name="dy_scales%d" % h, align_bytes=64) for h in range(2)]
@@ -105,24 +108,23 @@ def tile_list_embg_hl_noneP_kernel(tc, dy, w, wgo, offs, out_0, out_1, out_2):
 
         def product(r, h):
             acc[r, h] = psum.tile([P, HALF], F32, name="acc%d_%d" % (r, h))
-            cols = slice(r * P, (r + 1) * P)
-            for first, codes, scales in ((True, hi_codes, hi_scales), (False, lo_codes, lo_scales)):
+            for part in range(2):
                 nc.tensor.matmul_mx(
                     out=acc[r, h][:],
-                    lhsT=codes[:, cols].bitcast(E4M3),
-                    lhsT_scale=scales[:, cols],
+                    lhsT=w_codes[part, r].bitcast(E4M3),
+                    lhsT_scale=w_scales[:, part * N + r * P : part * N + (r + 1) * P],
                     rhs=dy_codes[h][:].bitcast(E5M2),
                     rhs_scale=dy_scales[h][:],
-                    start=first,
-                    stop=not first,
+                    start=part == 0,
+                    stop=part == 1,
                 )
 
-        def evacuate(r, j0, j1, tag):
+        def evacuate(r, j0, j1, tag, copy):
             dx = keep.tile([P, j1 - j0], F32, name="dx%d_%d" % (r, j0), tag=tag, align_bytes=64)
             for h in range(2):
                 a, b = max(j0, h * HALF), min(j1, (h + 1) * HALF)
                 if a < b:
-                    nc.scalar.copy(out=dx[:, a - j0 : b - j0], in_=acc[r, h][:, a - h * HALF : b - h * HALF])
+                    copy(out=dx[:, a - j0 : b - j0], in_=acc[r, h][:, a - h * HALF : b - h * HALF])
             return dx
 
         def scatter(r, j0, j1, dx):
@@ -135,38 +137,36 @@ def tile_list_embg_hl_noneP_kernel(tc, dy, w, wgo, offs, out_0, out_1, out_2):
         round_dy(0, nc.scalar.copy, "dy_bf0")
         quantize_dy(0)
         round_dy(1, nc.vector.tensor_copy, "dy_bf1")
-        quantize_w(0, 1)
+        first_codes = keep.tile([P, 2 * P], U32, name="first_codes", align_bytes=64)
+        quantize_w(0, 1, first_codes, 0)
         quantize_dy(1)
         product(0, 0)
-        dx_first = evacuate(0, 0, HALF, "first")
-        quantize_w(1, 2)
-        quantize_w(2, 4)
-        round_dy(2, nc.scalar.copy, "dy_bf1")
-        round_dy(3, nc.scalar.copy, "lo_bf")
+        rest_codes = keep.tile([P, 6 * P], U32, name="rest_codes", tag="dy_bf1", align_bytes=64)
+        quantize_w(1, 2, rest_codes, 0)
+        quantize_w(2, 4, rest_codes, 2 * P)
+        dx_first = evacuate(0, 0, PIECE, "first", nc.vector.tensor_copy)
+        round_dy(2, nc.scalar.copy, "dy_bf2")
+        round_dy(3, nc.scalar.copy, "dy_bf3")
+        dx_second = evacuate(0, PIECE, HALF, "second", nc.scalar.copy)
         for r in range(1, PACK):
             product(r, 0)
-        scatter(0, 0, HALF, dx_first)
+        scatter(0, 0, PIECE, dx_first)
         dy_codes.append(keep.tile([P, HALF], U32, name="dy_codes1", tag="first", align_bytes=64))
         quantize_dy(2)
-        dx_fill = evacuate(1, 0, PIECE, "dy_bf1")
         quantize_dy(3)
         for r in range(PACK):
             product(r, 1)
-        dx0 = evacuate(0, HALF, J, "slot2")
-        scatter(1, 0, PIECE, dx_fill)
-        dx1 = evacuate(1, PIECE, J, "slot3")
+        dx0 = evacuate(0, HALF, J, "slot2", nc.scalar.copy)
+        scatter(0, PIECE, HALF, dx_second)
+        dx1 = evacuate(1, 0, J, "slot3", nc.scalar.copy)
         scatter(0, HALF, J, dx0)
-        dx2 = evacuate(2, 0, J, "dx2")
-        dx3 = evacuate(3, 0, J, "dx3")
+        dx2 = evacuate(2, 0, J, "dx2", nc.scalar.copy)
+        dx3 = evacuate(3, 0, J, "dx3", nc.scalar.copy)
         nc.sync.dma_start(out=out_rows[:, 0, :], in_=page[0][:])
         nc.scalar.copy(out=y_bf[:, :, 0], in_=page[0][:])
-        page.append(keep.tile([P, T], F32, name="page2", tag="slot2", align_bytes=64))
-        nc.gpsimd.memset(page[2][:], 0.0)
-        scatter(1, PIECE, J, dx1)
+        scatter(1, 0, J, dx1)
         nc.sync.dma_start(out=out_rows[:, 1, :], in_=page[1][:])
         nc.scalar.copy(out=y_bf[:, :, 1], in_=page[1][:])
-        page.append(keep.tile([P, T], F32, name="page3", tag="slot3", align_bytes=64))
-        nc.gpsimd.memset(page[3][:], 0.0)
         scatter(2, 0, J, dx2)
         nc.sync.dma_start(out=out_rows[:, 2, :], in_=page[2][:])
         split = VECTOR_CHUNKS * CHUNK
@@ -201,12 +201,13 @@ def tile_list_embg_hl_noneP_kernel(tc, dy, w, wgo, offs, out_0, out_1, out_2):
         for c in range(1, VECTOR_CHUNKS):
             round_last(c, nc.vector.tensor_copy)
             quantize_y(c - 1)
-            if c % 2 == 0:
-                store_words(c - 2, c)
-        quantize_y(5)
+        store_words(0, 2)
         quantize_y(4)
+        quantize_y(3)
+        quantize_y(5)
+        store_words(2, 5)
         quantize_y(6)
-        store_words(4, 7)
+        store_words(5, 7)
         quantize_y(7)
         store_words(7, 8)
         for q in range(4):

@@ -17,12 +17,15 @@ ALU = mybir.AluOpType
 
 P = 128
 PACK = 4
+GROUP = 16
 HALF = 512
 PIECE = 256
+BLOCK = 128
 HI_MASK = -(1 << 20)
 CHUNK = 256
 CHUNKS = T // CHUNK
-VECTOR_CHUNKS = 4
+VECTOR_CHUNKS = CHUNKS // 2
+QUADRANTS = 4
 
 
 def tile_list_embg_hl_noneP_kernel(tc, dy, w, wgo, offs, out_0, out_1, out_2):
@@ -35,72 +38,82 @@ def tile_list_embg_hl_noneP_kernel(tc, dy, w, wgo, offs, out_0, out_1, out_2):
         dy_rows = dy.rearrange("(p i) j -> p i j", i=PACK)
         out_rows = out_0.rearrange("(p r) t -> p r t", r=PACK)
 
-        offsets = keep.tile([P, J // 16], U16, name="offsets")
-        w_raw = [keep.tile([P, PACK, PIECE], F32, name="w_raw%d" % a) for a in range(2)]
-        dy_raw = [keep.tile([P, PACK, PIECE], F32, name="dy_raw%d" % a) for a in range(4)]
+        offsets = keep.tile([P, J // GROUP], U16, name="offsets")
+        w_raw = [keep.tile([P, PACK, PIECE], F32, name="w_raw%d" % a) for a in range(N // PIECE)]
+        dy_raw = [keep.tile([P, PACK, PIECE], F32, name="dy_raw%d" % a) for a in range(J // PIECE)]
         weight = keep.tile([P, J], F32, name="weight")
-
-        for a in range(2):
+        for a in range(N // PIECE):
             nc.sync.dma_start(out=w_raw[a][:], in_=w_rows[:, :, a * PIECE : (a + 1) * PIECE])
-        for a in range(2):
+        for a in range(J // PIECE):
             nc.sync.dma_start(out=dy_raw[a][:], in_=dy_rows[:, :, a * PIECE : (a + 1) * PIECE])
         nc.sync.dma_start(offsets[:], offs)
-        nc.sync.dma_start(out=weight[:, :PIECE], in_=wgo[:, :PIECE])
-        for a in range(2, 4):
-            nc.sync.dma_start(out=dy_raw[a][:], in_=dy_rows[:, :, a * PIECE : (a + 1) * PIECE])
-        nc.sync.dma_start(out=weight[:, PIECE:], in_=wgo[:, PIECE:])
+        for h in range(J // HALF):
+            nc.sync.dma_start(out=weight[:, h * HALF : (h + 1) * HALF], in_=wgo[:, h * HALF : (h + 1) * HALF])
 
-        page = [keep.tile([P, T], F32, name="page%d" % r) for r in range(4)]
-        for r in range(4):
-            nc.vector.memset(page[r][:], 0.0)
-
+        page = [keep.tile([P, T], F32, name="page0")]
+        nc.vector.memset(page[0][:], 0.0)
 
         hi_bf = keep.tile([P, PACK, P, PACK], BF16, name="hi_bf", align_bytes=64)
-        lo_bf = keep.tile([P, PACK, P, PACK], BF16, name="lo_bf", tag="lo_bf", align_bytes=64)
-        for a in range(2):
-            hi = keep.tile([P, PACK, PIECE], F32, name="hi%d" % a)
+        lo_bf = keep.tile([P, PACK, P, PACK], BF16, name="lo_bf", align_bytes=64)
+        hi = [keep.tile([P, PACK, BLOCK], F32, name="hi%d" % b) for b in range(N // BLOCK)]
+
+        def w_block(b):
+            a, first = divmod(b * BLOCK, PIECE)
+            return w_raw[a][:, :, first : first + BLOCK]
+
+        def dealt(tile, b):
+            return tile[:, :, b * BLOCK // PACK : (b + 1) * BLOCK // PACK, :].rearrange("p r m i -> p m i r")
+
+        def mask(b):
             nc.vector.tensor_scalar(
-                out=hi[:].bitcast(I32), in0=w_raw[a][:].bitcast(I32), scalar1=HI_MASK, scalar2=None, op0=ALU.bitwise_and
+                out=hi[b][:].bitcast(I32), in0=w_block(b).bitcast(I32), scalar1=HI_MASK, scalar2=None, op0=ALU.bitwise_and
             )
-            ms = slice(a * PIECE // PACK, (a + 1) * PIECE // PACK)
-            hi_src = hi[:].rearrange("p i (m r) -> p m i r", r=PACK)
-            w_src = w_raw[a][:].rearrange("p i (m r) -> p m i r", r=PACK)
-            nc.scalar.copy(out=hi_bf[:, :, ms, :].rearrange("p r m i -> p m i r"), in_=hi_src)
+            nc.scalar.copy(out=dealt(hi_bf, b), in_=hi[b][:].rearrange("p i (m r) -> p m i r", r=PACK))
+
+        def subtract(b):
             nc.vector.tensor_tensor(
-                out=lo_bf[:, :, ms, :].rearrange("p r m i -> p m i r"), in0=w_src, in1=hi_src, op=ALU.subtract
+                out=dealt(lo_bf, b),
+                in0=w_block(b).rearrange("p i (m r) -> p m i r", r=PACK),
+                in1=hi[b][:].rearrange("p i (m r) -> p m i r", r=PACK),
+                op=ALU.subtract,
             )
+
+        mask(0)
+        mask(1)
+        subtract(0)
+        mask(2)
+        mask(3)
+        for b in range(1, N // BLOCK):
+            subtract(b)
 
         w_codes = {}
         w_scales = keep.tile([P, 2 * N], U8, name="w_scales", align_bytes=64)
 
-        def quantize_w(r0, r1, codes, first):
-            for part, src in enumerate((hi_bf, lo_bf)):
-                at = first + part * (r1 - r0) * P
-                plane = part * N + r0 * P
-                nc.vector.quantize_mx(
-                    out=codes[:, at : at + (r1 - r0) * P].bitcast(E4M3),
-                    scales=w_scales[:, plane : plane + (r1 - r0) * P],
-                    in_=src[:, r0:r1, :, :].rearrange("p r m i -> p (r m i)"),
-                )
-                for r in range(r0, r1):
-                    w_codes[part, r] = codes[:, at + (r - r0) * P : at + (r - r0 + 1) * P]
+        def quantize_w(part, r0, r1, codes):
+            first = part * N + r0 * P
+            nc.vector.quantize_mx(
+                out=codes.bitcast(E4M3),
+                scales=w_scales[:, first : first + (r1 - r0) * P],
+                in_=(hi_bf, lo_bf)[part][:, r0:r1, :, :].rearrange("p r m i -> p (r m i)"),
+            )
+            for r in range(r0, r1):
+                w_codes[part, r] = codes[:, (r - r0) * P : (r - r0 + 1) * P]
 
-        dy_codes = [keep.tile([P, HALF], U32, name="dy_codes0", align_bytes=64)]
-        dy_scales = [keep.tile([P, HALF], U8, name="dy_scales%d" % h, align_bytes=64) for h in range(2)]
-        dy_bf = {}
+        dy_codes = [keep.tile([P, HALF], U32, name="dy_codes%d" % h, align_bytes=64) for h in range(J // HALF)]
+        dy_scales = [keep.tile([P, HALF], U8, name="dy_scales%d" % h, align_bytes=64) for h in range(J // HALF)]
+        dy_bf = [keep.tile([P, PIECE, PACK], BF16, name="dy_bf%d" % a, align_bytes=64) for a in range(J // PIECE)]
 
-        def round_dy(a, copy, tag):
-            dy_bf[a] = keep.tile([P, PIECE, PACK], BF16, name="dy_bf%d" % a, tag=tag, align_bytes=64)
+        def round_dy(a, copy):
             copy(
                 out=dy_bf[a][:].rearrange("p (c e) i -> p c i e", e=4),
                 in_=dy_raw[a][:].rearrange("p i (c e) -> p c i e", e=4),
             )
 
         def quantize_dy(a):
-            cols = slice((a % 2) * PIECE, (a % 2 + 1) * PIECE)
+            h, first = divmod(a * PIECE, HALF)
             nc.vector.quantize_mx(
-                out=dy_codes[a // 2][:, cols].bitcast(E5M2),
-                scales=dy_scales[a // 2][:, cols],
+                out=dy_codes[h][:, first : first + PIECE].bitcast(E5M2),
+                scales=dy_scales[h][:, first : first + PIECE],
                 in_=dy_bf[a][:].rearrange("p c i -> p (c i)"),
             )
 
@@ -119,54 +132,60 @@ def tile_list_embg_hl_noneP_kernel(tc, dy, w, wgo, offs, out_0, out_1, out_2):
                     stop=part == 1,
                 )
 
-        def evacuate(r, j0, j1, tag, copy):
-            dx = keep.tile([P, j1 - j0], F32, name="dx%d_%d" % (r, j0), tag=tag, align_bytes=64)
-            for h in range(2):
-                a, b = max(j0, h * HALF), min(j1, (h + 1) * HALF)
-                if a < b:
-                    copy(out=dx[:, a - j0 : b - j0], in_=acc[r, h][:, a - h * HALF : b - h * HALF])
+        def evacuate(r, halves, tag):
+            dx = keep.tile([P, len(halves) * HALF], F32, name="dx%d_%d" % (r, halves[0]), tag=tag, align_bytes=64)
+            for at, h in enumerate(halves):
+                nc.scalar.copy(out=dx[:, at * HALF : (at + 1) * HALF], in_=acc[r, h][:])
             return dx
 
         def scatter(r, j0, j1, dx):
             nc.vector.tensor_tensor(
-                page[r][:].indirect(offsets[:, j0 // 16 : j1 // 16]), dx[:], weight[:, j0:j1], ALU.mult
+                page[r][:].indirect(offsets[:, j0 // GROUP : j1 // GROUP]), dx[:], weight[:, j0:j1], ALU.mult
             )
+
+        def clear_page(r):
+            page.append(keep.tile([P, T], F32, name="page%d" % r, tag="before_page%d" % r, align_bytes=64))
+            nc.gpsimd.memset(page[r][:], 0.0)
 
         y_bf = keep.tile([P, T, PACK], BF16, name="y_bf", align_bytes=64)
 
-        round_dy(0, nc.scalar.copy, "dy_bf0")
-        quantize_dy(0)
-        round_dy(1, nc.vector.tensor_copy, "dy_bf1")
-        first_codes = keep.tile([P, 2 * P], U32, name="first_codes", align_bytes=64)
-        quantize_w(0, 1, first_codes, 0)
+        round_dy(0, nc.scalar.copy)
+        round_dy(1, nc.vector.tensor_copy)
+        first_codes = keep.tile([P, 2, P], U32, name="first_codes", align_bytes=64)
+        quantize_w(0, 0, 1, first_codes[:, 0, :])
         quantize_dy(1)
+        quantize_dy(0)
+        quantize_w(1, 0, 1, first_codes[:, 1, :])
         product(0, 0)
-        rest_codes = keep.tile([P, 6 * P], U32, name="rest_codes", tag="dy_bf1", align_bytes=64)
-        quantize_w(1, 2, rest_codes, 0)
-        quantize_w(2, 4, rest_codes, 2 * P)
-        dx_first = evacuate(0, 0, PIECE, "first", nc.vector.tensor_copy)
-        round_dy(2, nc.scalar.copy, "dy_bf2")
-        round_dy(3, nc.scalar.copy, "dy_bf3")
-        dx_second = evacuate(0, PIECE, HALF, "second", nc.scalar.copy)
-        for r in range(1, PACK):
-            product(r, 0)
-        scatter(0, 0, PIECE, dx_first)
-        dy_codes.append(keep.tile([P, HALF], U32, name="dy_codes1", tag="first", align_bytes=64))
+
+        rest_codes = keep.tile([P, 2, (PACK - 1) * P], U32, name="rest_codes", tag="dy_bf0", align_bytes=64)
+        for r0, r1 in ((1, 2), (2, PACK)):
+            for part in range(2):
+                quantize_w(part, r0, r1, rest_codes[:, part, (r0 - 1) * P : (r1 - 1) * P])
+        round_dy(2, nc.scalar.copy)
+        round_dy(3, nc.scalar.copy)
+        dx_first = evacuate(0, [0], "before_page1")
         quantize_dy(2)
         quantize_dy(3)
-        for r in range(PACK):
-            product(r, 1)
-        dx0 = evacuate(0, HALF, J, "slot2", nc.scalar.copy)
-        scatter(0, PIECE, HALF, dx_second)
-        dx1 = evacuate(1, 0, J, "slot3", nc.scalar.copy)
-        scatter(0, HALF, J, dx0)
-        dx2 = evacuate(2, 0, J, "dx2", nc.scalar.copy)
-        dx3 = evacuate(3, 0, J, "dx3", nc.scalar.copy)
+        product(0, 1)
+        for r in range(1, PACK):
+            for h in range(J // HALF):
+                product(r, h)
+
+        scatter(0, 0, HALF, dx_first)
+        dx_second = evacuate(0, [1], "before_page2")
+        clear_page(1)
+        dx1 = evacuate(1, [0, 1], "before_page3")
+        scatter(0, HALF, J, dx_second)
+        dx2 = evacuate(2, [0, 1], "dx2")
+        dx3 = evacuate(3, [0, 1], "dx3")
         nc.sync.dma_start(out=out_rows[:, 0, :], in_=page[0][:])
         nc.scalar.copy(out=y_bf[:, :, 0], in_=page[0][:])
+        clear_page(2)
         scatter(1, 0, J, dx1)
         nc.sync.dma_start(out=out_rows[:, 1, :], in_=page[1][:])
         nc.scalar.copy(out=y_bf[:, :, 1], in_=page[1][:])
+        clear_page(3)
         scatter(2, 0, J, dx2)
         nc.sync.dma_start(out=out_rows[:, 2, :], in_=page[2][:])
         split = VECTOR_CHUNKS * CHUNK
@@ -176,10 +195,10 @@ def tile_list_embg_hl_noneP_kernel(tc, dy, w, wgo, offs, out_0, out_1, out_2):
         nc.sync.dma_start(out=out_rows[:, 3, :], in_=page[3][:])
 
         y_codes = keep.tile([P, T], U32, name="y_codes", align_bytes=64)
-        y_scales = keep.tile([P, T], U8, name="y_scales", align_bytes=64)
+        y_scales = keep.tile([P, 2 * CHUNK], U8, name="y_scales", align_bytes=64)
         words = out_1[0].rearrange("p t i -> p (t i)").bitcast(I32)
 
-        def round_last(c, copy):
+        def round_last_page(c, copy):
             cols = slice(c * CHUNK, (c + 1) * CHUNK)
             copy(out=y_bf[:, cols, 3], in_=page[3][:, cols])
 
@@ -187,7 +206,7 @@ def tile_list_embg_hl_noneP_kernel(tc, dy, w, wgo, offs, out_0, out_1, out_2):
             cols = slice(c * CHUNK, (c + 1) * CHUNK)
             nc.vector.quantize_mx(
                 out=y_codes[:, cols].bitcast(E4M3),
-                scales=y_scales[:, cols],
+                scales=y_scales[4 * (c // 2) :, (c % 2) * CHUNK : (c % 2 + 1) * CHUNK],
                 in_=y_bf[:, cols, :].rearrange("p t i -> p (t i)"),
             )
 
@@ -196,22 +215,20 @@ def tile_list_embg_hl_noneP_kernel(tc, dy, w, wgo, offs, out_0, out_1, out_2):
             nc.sync.dma_start(out=words[:, cols], in_=y_codes[:, cols].bitcast(I32))
 
         for c in range(VECTOR_CHUNKS, CHUNKS):
-            round_last(c, nc.scalar.copy)
-        round_last(0, nc.vector.tensor_copy)
-        for c in range(1, VECTOR_CHUNKS):
-            round_last(c, nc.vector.tensor_copy)
-            quantize_y(c - 1)
-        store_words(0, 2)
-        quantize_y(4)
-        quantize_y(3)
-        quantize_y(5)
-        store_words(2, 5)
-        quantize_y(6)
-        store_words(5, 7)
-        quantize_y(7)
-        store_words(7, 8)
-        for q in range(4):
-            queue = nc.scalar if q % 2 else nc.sync
+            round_last_page(c, nc.scalar.copy)
+        round_last_page(0, nc.vector.tensor_copy)
+        for c in range(CHUNKS):
+            if c + 1 < VECTOR_CHUNKS:
+                round_last_page(c + 1, nc.vector.tensor_copy)
+            quantize_y(c)
+            if c >= CHUNKS - 2:
+                store_words(c, c + 1)
+            elif c % 2:
+                store_words(c - 1, c + 1)
+
+        for q in range(QUADRANTS):
+            queue = nc.sync if q % 2 else nc.scalar
             queue.dma_start(
-                out=out_2[0, 4 * q : 4 * q + 4, :].bitcast(I32), in_=y_scales[32 * q : 32 * q + 4, :].bitcast(I32)
+                out=out_2[0, 4 * q : 4 * q + 4, :].bitcast(I32).rearrange("s (g x) -> g s x", g=CHUNKS // 2),
+                in_=y_scales[32 * q : 32 * q + 16, :].bitcast(I32),
             )

@@ -1,6 +1,7 @@
 from contextlib import ExitStack
 
 import concourse.mybir as mybir
+from concourse.masks import make_identity
 
 K, N, T, J = 512, 512, 2048, 1024
 FLOPS = 2 * 2 * K * N * J
@@ -20,11 +21,12 @@ PACK = 4
 GROUP = 16
 HALF = 512
 PIECE = 256
-BLOCK = 128
+WORDS = PIECE // PACK
 HI_MASK = -(1 << 20)
 CHUNK = 256
 CHUNKS = T // CHUNK
 VECTOR_CHUNKS = CHUNKS // 2
+SPLIT = VECTOR_CHUNKS * CHUNK
 QUADRANTS = 4
 
 
@@ -40,72 +42,82 @@ def tile_list_embg_hl_noneP_kernel(tc, dy, w, wgo, offs, out_0, out_1, out_2):
 
         offsets = keep.tile([P, J // GROUP], U16, name="offsets")
         w_raw = [keep.tile([P, PACK, PIECE], F32, name="w_raw%d" % a) for a in range(N // PIECE)]
-        dy_raw = [keep.tile([P, PACK, PIECE], F32, name="dy_raw%d" % a) for a in range(J // PIECE)]
+        dy_raw = [
+            keep.tile([P, PACK, PIECE], F32, name="dy_raw%d" % a, tag="dy_raw%d" % a, align_bytes=64)
+            for a in range(J // PIECE)
+        ]
         weight = keep.tile([P, J], F32, name="weight")
-        for a in range(N // PIECE):
+
+        def load_w(a):
             nc.sync.dma_start(out=w_raw[a][:], in_=w_rows[:, :, a * PIECE : (a + 1) * PIECE])
-        for a in range(J // PIECE):
+
+        def load_dy(a):
             nc.sync.dma_start(out=dy_raw[a][:], in_=dy_rows[:, :, a * PIECE : (a + 1) * PIECE])
-        nc.sync.dma_start(offsets[:], offs)
-        for h in range(J // HALF):
+
+        def load_weight(h):
             nc.sync.dma_start(out=weight[:, h * HALF : (h + 1) * HALF], in_=wgo[:, h * HALF : (h + 1) * HALF])
 
-        page = [keep.tile([P, T], F32, name="page0")]
+        load_w(0)
+        load_dy(0)
+        load_dy(1)
+        load_w(1)
+        nc.sync.dma_start(offsets[:], offs)
+        load_weight(0)
+        load_dy(2)
+        load_dy(3)
+        load_weight(1)
+
+        page = {}
+        page[0] = keep.tile([P, T], F32, name="page0")
         nc.vector.memset(page[0][:], 0.0)
+        identity = keep.tile([P, P], F32, name="identity")
+        make_identity(nc, identity[:])
+        page[1] = keep.tile([P, T], F32, name="page1")
+        nc.gpsimd.memset(page[1][:], 0.0)
 
-        hi_bf = keep.tile([P, PACK, P, PACK], BF16, name="hi_bf", align_bytes=64)
-        lo_bf = keep.tile([P, PACK, P, PACK], BF16, name="lo_bf", align_bytes=64)
-        hi = [keep.tile([P, PACK, BLOCK], F32, name="hi%d" % b) for b in range(N // BLOCK)]
+        width = PIECE * PACK
+        late_bf = keep.tile([P, 4 * width], BF16, name="late_bf", tag="late", align_bytes=64)
+        early = [keep.tile([P, width], BF16, name="early%d" % a, align_bytes=64) for a in range(4)]
+        dy_bf = [early[0][:], early[1][:], late_bf[:, 0:width], late_bf[:, width : 2 * width]]
+        w_bf = [early[2][:], early[3][:], late_bf[:, 2 * width : 3 * width], late_bf[:, 3 * width : 4 * width]]
+        hi = [keep.tile([P, PACK, PIECE], F32, name="hi%d" % a) for a in range(N // PIECE)]
 
-        def w_block(b):
-            a, first = divmod(b * BLOCK, PIECE)
-            return w_raw[a][:, :, first : first + BLOCK]
+        def slots(tile, pair):
+            return tile[:].rearrange("p i (q r) -> p q i r", r=PACK)[:, :, :, 2 * pair : 2 * pair + 2]
 
-        def dealt(tile, b):
-            return tile[:, :, b * BLOCK // PACK : (b + 1) * BLOCK // PACK, :].rearrange("p r m i -> p m i r")
+        def dealt(a, pair, part):
+            if pair == 0:
+                return w_bf[a].rearrange("p (s q b i) -> p s q i b", s=2, b=2, i=PACK)[:, part]
+            both = late_bf[:, 2 * width :].rearrange("p (b s m i) -> p s m i b", b=2, s=2, i=PACK)
+            return both[:, part, a * WORDS : (a + 1) * WORDS]
 
-        def mask(b):
+        def mask(a):
             nc.vector.tensor_scalar(
-                out=hi[b][:].bitcast(I32), in0=w_block(b).bitcast(I32), scalar1=HI_MASK, scalar2=None, op0=ALU.bitwise_and
-            )
-            nc.scalar.copy(out=dealt(hi_bf, b), in_=hi[b][:].rearrange("p i (m r) -> p m i r", r=PACK))
-
-        def subtract(b):
-            nc.vector.tensor_tensor(
-                out=dealt(lo_bf, b),
-                in0=w_block(b).rearrange("p i (m r) -> p m i r", r=PACK),
-                in1=hi[b][:].rearrange("p i (m r) -> p m i r", r=PACK),
-                op=ALU.subtract,
+                out=hi[a][:].bitcast(I32), in0=w_raw[a][:].bitcast(I32), scalar1=HI_MASK, scalar2=None, op0=ALU.bitwise_and
             )
 
-        mask(0)
-        mask(1)
-        subtract(0)
-        mask(2)
-        mask(3)
-        for b in range(1, N // BLOCK):
-            subtract(b)
+        def round_hi(a, pair):
+            nc.scalar.copy(out=dealt(a, pair, 0), in_=slots(hi[a], pair))
 
-        w_codes = {}
-        w_scales = keep.tile([P, 2 * N], U8, name="w_scales", align_bytes=64)
+        def subtract(a, pair):
+            nc.vector.tensor_tensor(out=dealt(a, pair, 1), in0=slots(w_raw[a], pair), in1=slots(hi[a], pair), op=ALU.subtract)
 
-        def quantize_w(part, r0, r1, codes):
-            first = part * N + r0 * P
-            nc.vector.quantize_mx(
-                out=codes.bitcast(E4M3),
-                scales=w_scales[:, first : first + (r1 - r0) * P],
-                in_=(hi_bf, lo_bf)[part][:, r0:r1, :, :].rearrange("p r m i -> p (r m i)"),
-            )
-            for r in range(r0, r1):
-                w_codes[part, r] = codes[:, (r - r0) * P : (r - r0 + 1) * P]
+        w_codes, w_scales = {}, {}
+
+        def quantize_w(g0, g1, values):
+            codes = keep.tile([P, (g1 - g0) * 2 * P], U32, name="w_codes%d" % g0, align_bytes=64)
+            scales = keep.tile([P, (g1 - g0) * 2 * P], U8, name="w_scales%d" % g0, align_bytes=64)
+            nc.vector.quantize_mx(out=codes[:].bitcast(E4M3), scales=scales[:], in_=values)
+            for g in range(g0, g1):
+                cols = slice((g - g0) * 2 * P, (g - g0 + 1) * 2 * P)
+                w_codes[g], w_scales[g] = codes[:, cols], scales[:, cols]
 
         dy_codes = [keep.tile([P, HALF], U32, name="dy_codes%d" % h, align_bytes=64) for h in range(J // HALF)]
         dy_scales = [keep.tile([P, HALF], U8, name="dy_scales%d" % h, align_bytes=64) for h in range(J // HALF)]
-        dy_bf = [keep.tile([P, PIECE, PACK], BF16, name="dy_bf%d" % a, align_bytes=64) for a in range(J // PIECE)]
 
         def round_dy(a, copy):
             copy(
-                out=dy_bf[a][:].rearrange("p (c e) i -> p c i e", e=4),
+                out=dy_bf[a].rearrange("p (c e i) -> p c i e", e=4, i=PACK),
                 in_=dy_raw[a][:].rearrange("p i (c e) -> p c i e", e=4),
             )
 
@@ -114,83 +126,111 @@ def tile_list_embg_hl_noneP_kernel(tc, dy, w, wgo, offs, out_0, out_1, out_2):
             nc.vector.quantize_mx(
                 out=dy_codes[h][:, first : first + PIECE].bitcast(E5M2),
                 scales=dy_scales[h][:, first : first + PIECE],
-                in_=dy_bf[a][:].rearrange("p c i -> p (c i)"),
+                in_=dy_bf[a],
             )
 
+        bank = {(0, 0): 0, (1, 0): 1, (0, 1): 2, (1, 1): 3, (2, 0): 1, (2, 1): 0, (3, 0): 2, (3, 1): 3}
         acc = {}
 
-        def product(r, h):
-            acc[r, h] = psum.tile([P, HALF], F32, name="acc%d_%d" % (r, h))
+        def product(g, h):
+            acc[g, h] = psum.tile([P, HALF], F32, name="acc%d_%d" % (g, h), tag="bank%d" % bank[g, h])
             for part in range(2):
                 nc.tensor.matmul_mx(
-                    out=acc[r, h][:],
-                    lhsT=w_codes[part, r].bitcast(E4M3),
-                    lhsT_scale=w_scales[:, part * N + r * P : part * N + (r + 1) * P],
+                    out=acc[g, h][:],
+                    lhsT=w_codes[g][:, part * P : (part + 1) * P].bitcast(E4M3),
+                    lhsT_scale=w_scales[g][:, part * P : (part + 1) * P],
                     rhs=dy_codes[h][:].bitcast(E5M2),
                     rhs_scale=dy_scales[h][:],
                     start=part == 0,
                     stop=part == 1,
                 )
 
-        def evacuate(r, halves, tag):
-            dx = keep.tile([P, len(halves) * HALF], F32, name="dx%d_%d" % (r, halves[0]), tag=tag, align_bytes=64)
+        def evacuate(g, halves, tag):
+            dx = keep.tile([P, len(halves) * HALF], F32, name="dx%d_%d" % (g, halves[0]), tag=tag, align_bytes=64)
             for at, h in enumerate(halves):
-                nc.scalar.copy(out=dx[:, at * HALF : (at + 1) * HALF], in_=acc[r, h][:])
-            return dx
+                nc.scalar.copy(out=dx[:, at * HALF : (at + 1) * HALF], in_=acc[g, h][:])
+            return dx[:]
 
-        def scatter(r, j0, j1, dx):
+        def scatter(g, j0, j1, dx):
             nc.vector.tensor_tensor(
-                page[r][:].indirect(offsets[:, j0 // GROUP : j1 // GROUP]), dx[:], weight[:, j0:j1], ALU.mult
+                page[g][:].indirect(offsets[:, j0 // GROUP : j1 // GROUP]), dx, weight[:, j0:j1], ALU.mult
             )
 
-        def clear_page(r):
-            page.append(keep.tile([P, T], F32, name="page%d" % r, tag="before_page%d" % r, align_bytes=64))
-            nc.gpsimd.memset(page[r][:], 0.0)
+        def clear_page(g, tag):
+            page[g] = keep.tile([P, T], F32, name="page%d" % g, tag=tag, align_bytes=64)
+            nc.gpsimd.memset(page[g][:], 0.0)
 
-        y_bf = keep.tile([P, T, PACK], BF16, name="y_bf", align_bytes=64)
-
+        mask(0)
+        round_hi(0, 0)
+        subtract(0, 0)
         round_dy(0, nc.scalar.copy)
+        subtract(0, 1)
+        quantize_w(0, 1, w_bf[0])
         round_dy(1, nc.vector.tensor_copy)
-        first_codes = keep.tile([P, 2, P], U32, name="first_codes", align_bytes=64)
-        quantize_w(0, 0, 1, first_codes[:, 0, :])
-        quantize_dy(1)
         quantize_dy(0)
-        quantize_w(1, 0, 1, first_codes[:, 1, :])
+        quantize_dy(1)
         product(0, 0)
-
-        rest_codes = keep.tile([P, 2, (PACK - 1) * P], U32, name="rest_codes", tag="dy_bf0", align_bytes=64)
-        for r0, r1 in ((1, 2), (2, PACK)):
-            for part in range(2):
-                quantize_w(part, r0, r1, rest_codes[:, part, (r0 - 1) * P : (r1 - 1) * P])
+        dx00 = evacuate(0, [0], "dx00")
+        scatter(0, 0, HALF, dx00)
+        round_hi(0, 1)
+        mask(1)
+        round_hi(1, 0)
+        subtract(1, 0)
+        round_hi(1, 1)
+        subtract(1, 1)
+        quantize_w(1, 2, w_bf[1])
+        product(1, 0)
         round_dy(2, nc.scalar.copy)
         round_dy(3, nc.scalar.copy)
-        dx_first = evacuate(0, [0], "before_page1")
-        quantize_dy(2)
-        quantize_dy(3)
+        nc.vector.quantize_mx(out=dy_codes[1][:].bitcast(E5M2), scales=dy_scales[1][:], in_=late_bf[:, : 2 * width])
+        quantize_w(2, 4, late_bf[:, 2 * width :])
         product(0, 1)
-        for r in range(1, PACK):
+        product(1, 1)
+        dx10 = dy_raw[3][:].rearrange("p i c -> p (i c)")[:, :HALF]
+        nc.scalar.copy(out=dx10, in_=acc[1, 0][:])
+        clear_page(2, "late")
+        scatter(1, 0, HALF, dx10)
+        dx01 = evacuate(0, [1], "dx01")
+        dx11 = evacuate(1, [1], "dx11")
+        for g in range(2, PACK):
             for h in range(J // HALF):
-                product(r, h)
-
-        scatter(0, 0, HALF, dx_first)
-        dx_second = evacuate(0, [1], "before_page2")
-        clear_page(1)
-        dx1 = evacuate(1, [0, 1], "before_page3")
-        scatter(0, HALF, J, dx_second)
+                product(g, h)
         dx2 = evacuate(2, [0, 1], "dx2")
         dx3 = evacuate(3, [0, 1], "dx3")
-        nc.sync.dma_start(out=out_rows[:, 0, :], in_=page[0][:])
-        nc.scalar.copy(out=y_bf[:, :, 0], in_=page[0][:])
-        clear_page(2)
-        scatter(1, 0, J, dx1)
-        nc.sync.dma_start(out=out_rows[:, 1, :], in_=page[1][:])
-        nc.scalar.copy(out=y_bf[:, :, 1], in_=page[1][:])
-        clear_page(3)
+        clear_page(3, "dy_raw3")
+
+        y_bf = keep.tile([P, T, PACK], BF16, name="y_bf", align_bytes=64)
+        runs = T // HALF
+        pairs = [keep.tile([P, PACK, 2 * P], BF16, name="pairs%d" % c, align_bytes=64) for c in range(runs)]
+
+        def turn(g):
+            nc.sync.dma_start(out=out_rows[g * WORDS : (g + 1) * WORDS, 0:2, :], in_=page[g][:])
+            for c in range(runs):
+                turned = psum.tile([P, PACK, P], F32, name="turned%d_%d" % (g, c), tag="bank%d" % c)
+                for u in range(PACK):
+                    first = c * HALF + u * P
+                    nc.tensor.transpose(turned[:, u, :], page[g][:, first : first + P], identity[:])
+                nc.scalar.copy(out=pairs[c][:, :, g * P : (g + 1) * P], in_=turned[:])
+
+        def turn_back(c):
+            back = psum.tile([P, HALF], F32, name="back%d" % c, tag="bank%d" % c)
+            for u in range(PACK):
+                nc.tensor.transpose(back[:, u * P : (u + 1) * P], pairs[c][:, u, :].bitcast(F32), identity[:])
+            nc.scalar.copy(
+                out=y_bf[:, c * HALF : (c + 1) * HALF, :].bitcast(F32),
+                in_=back[:].unsqueeze(2).to_broadcast([P, HALF, 2]),
+            )
+
+        scatter(0, HALF, J, dx01)
+        turn(0)
+        scatter(1, HALF, J, dx11)
+        turn(1)
+        for c in range(runs):
+            turn_back(c)
         scatter(2, 0, J, dx2)
         nc.sync.dma_start(out=out_rows[:, 2, :], in_=page[2][:])
-        split = VECTOR_CHUNKS * CHUNK
-        nc.scalar.copy(out=y_bf[:, :split, 2:4], in_=page[2][:, :split].unsqueeze(2).to_broadcast([P, split, 2]))
-        nc.scalar.copy(out=y_bf[:, split:, 2], in_=page[2][:, split:])
+        nc.scalar.copy(out=y_bf[:, :SPLIT, 2:4], in_=page[2][:, :SPLIT].unsqueeze(2).to_broadcast([P, SPLIT, 2]))
+        nc.scalar.copy(out=y_bf[:, SPLIT:, 2], in_=page[2][:, SPLIT:])
         scatter(3, 0, J, dx3)
         nc.sync.dma_start(out=out_rows[:, 3, :], in_=page[3][:])
 

@@ -69,7 +69,8 @@ def tile_list_embg_hl_noneP_kernel(tc, dy, w, wgo, offs, out_0, out_1, out_2):
 
         page = {}
         page[0] = keep.tile([P, T], F32, name="page0")
-        nc.vector.memset(page[0][:], 0.0)
+        nc.vector.memset(page[0][:, : T - 1], 0.0)
+        nc.vector.memset(page[0][:, T - 1 :], 0.0)
         identity = keep.tile([P, P], F32, name="identity")
         make_identity(nc, identity[:])
         page[1] = keep.tile([P, T], F32, name="page1")

@@ -42,27 +42,24 @@ def tile_list_embg_hl_noneP_kernel(tc, dy, w, wgo, offs, out_0, out_1, out_2):
 
         offsets = keep.tile([P, J // GROUP], U16, name="offsets")
         w_raw = [keep.tile([P, PACK, PIECE], F32, name="w_raw%d" % a) for a in range(N // PIECE)]
-        dy_raw = [
-            keep.tile([P, PACK, PIECE], F32, name="dy_raw%d" % a, tag="dy_raw%d" % a, align_bytes=64)
-            for a in range(J // PIECE)
-        ]
+        dy_raw = [keep.tile([P, PACK * PIECE], F32, name="dy_raw%d" % a, align_bytes=64) for a in range(J // PIECE)]
         weight = keep.tile([P, J], F32, name="weight")
 
         def load_w(a):
             nc.sync.dma_start(out=w_raw[a][:], in_=w_rows[:, :, a * PIECE : (a + 1) * PIECE])
 
         def load_dy(a):
-            nc.sync.dma_start(out=dy_raw[a][:], in_=dy_rows[:, :, a * PIECE : (a + 1) * PIECE])
+            nc.sync.dma_start(out=dy_raw[a][:].rearrange("p (i c) -> p i c", i=PACK), in_=dy_rows[:, :, a * PIECE : (a + 1) * PIECE])
 
         def load_weight(h):
             nc.sync.dma_start(out=weight[:, h * HALF : (h + 1) * HALF], in_=wgo[:, h * HALF : (h + 1) * HALF])
 
         load_w(0)
         load_dy(0)
-        load_dy(1)
         load_w(1)
         nc.sync.dma_start(offsets[:], offs)
         load_weight(0)
+        load_dy(1)
         load_dy(2)
         load_dy(3)
         load_weight(1)
@@ -77,31 +74,45 @@ def tile_list_embg_hl_noneP_kernel(tc, dy, w, wgo, offs, out_0, out_1, out_2):
         nc.gpsimd.memset(page[1][:], 0.0)
 
         width = PIECE * PACK
-        late_bf = keep.tile([P, 4 * width], BF16, name="late_bf", tag="late", align_bytes=64)
-        early = [keep.tile([P, width], BF16, name="early%d" % a, align_bytes=64) for a in range(4)]
-        dy_bf = [early[0][:], early[1][:], late_bf[:, 0:width], late_bf[:, width : 2 * width]]
-        w_bf = [early[2][:], early[3][:], late_bf[:, 2 * width : 3 * width], late_bf[:, 3 * width : 4 * width]]
-        hi = [keep.tile([P, PACK, PIECE], F32, name="hi%d" % a) for a in range(N // PIECE)]
+        dy_bf = [keep.tile([P, width], BF16, name="dy_bf%d" % a, align_bytes=64) for a in range(J // PIECE)]
+        w_first = keep.tile([P, width], BF16, name="w_first", align_bytes=64)
+        w_bf = [w_first[:], dy_raw[0][:, :HALF].bitcast(BF16)]
+        w_late = keep.tile([P, 2 * width], BF16, name="w_late", align_bytes=64)
+        hi_own = [keep.tile([P, HALF], F32, name="hi%d" % a) for a in range(3)]
+        hi_flat = [tile[:] for tile in hi_own] + [dy_raw[0][:, HALF:]]
+        hi = {divmod(at, 2): flat.rearrange("p (i q b) -> p i q b", i=PACK, b=2) for at, flat in enumerate(hi_flat)}
 
-        def slots(tile, pair):
-            return tile[:].rearrange("p i (q r) -> p q i r", r=PACK)[:, :, :, 2 * pair : 2 * pair + 2]
+        def slots(ap, pair):
+            return ap.rearrange("p i (q r) -> p i q r", r=PACK)[:, :, :, 2 * pair : 2 * pair + 2]
 
         def dealt(a, pair, part):
             if pair == 0:
                 return w_bf[a].rearrange("p (s q b i) -> p s q i b", s=2, b=2, i=PACK)[:, part]
-            both = late_bf[:, 2 * width :].rearrange("p (b s m i) -> p s m i b", b=2, s=2, i=PACK)
+            both = w_late[:].rearrange("p (b s m i) -> p s m i b", b=2, s=2, i=PACK)
             return both[:, part, a * WORDS : (a + 1) * WORDS]
 
-        def mask(a):
+        def by_column(ap):
+            return ap.rearrange("p i q b -> p q i b")
+
+        def mask(a, pair):
             nc.vector.tensor_scalar(
-                out=hi[a][:].bitcast(I32), in0=w_raw[a][:].bitcast(I32), scalar1=HI_MASK, scalar2=None, op0=ALU.bitwise_and
+                out=hi_flat[2 * a + pair].bitcast(I32).rearrange("p (i q b) -> p i q b", i=PACK, b=2),
+                in0=slots(w_raw[a][:].bitcast(I32), pair),
+                scalar1=HI_MASK,
+                scalar2=None,
+                op0=ALU.bitwise_and,
             )
 
         def round_hi(a, pair):
-            nc.scalar.copy(out=dealt(a, pair, 0), in_=slots(hi[a], pair))
+            nc.scalar.copy(out=dealt(a, pair, 0), in_=by_column(hi[a, pair]))
 
         def subtract(a, pair):
-            nc.vector.tensor_tensor(out=dealt(a, pair, 1), in0=slots(w_raw[a], pair), in1=slots(hi[a], pair), op=ALU.subtract)
+            nc.vector.tensor_tensor(
+                out=dealt(a, pair, 1),
+                in0=by_column(slots(w_raw[a][:], pair)),
+                in1=by_column(hi[a, pair]),
+                op=ALU.subtract,
+            )
 
         w_codes, w_scales = {}, {}
 
@@ -113,44 +124,42 @@ def tile_list_embg_hl_noneP_kernel(tc, dy, w, wgo, offs, out_0, out_1, out_2):
                 cols = slice((g - g0) * 2 * P, (g - g0 + 1) * 2 * P)
                 w_codes[g], w_scales[g] = codes[:, cols], scales[:, cols]
 
-        dy_codes = [keep.tile([P, HALF], U32, name="dy_codes%d" % h, align_bytes=64) for h in range(J // HALF)]
-        dy_scales = [keep.tile([P, HALF], U8, name="dy_scales%d" % h, align_bytes=64) for h in range(J // HALF)]
+        dy_codes = keep.tile([P, J], U32, name="dy_codes", align_bytes=64)
+        dy_scales = keep.tile([P, J], U8, name="dy_scales", align_bytes=64)
 
-        def round_dy(a, copy):
-            copy(
-                out=dy_bf[a].rearrange("p (c e i) -> p c i e", e=4, i=PACK),
-                in_=dy_raw[a][:].rearrange("p i (c e) -> p c i e", e=4),
+        def round_dy(a):
+            nc.scalar.copy(
+                out=dy_bf[a][:].rearrange("p (c e i) -> p c i e", e=4, i=PACK),
+                in_=dy_raw[a][:].rearrange("p (i c e) -> p c i e", e=4, i=PACK),
             )
 
         def quantize_dy(a):
-            h, first = divmod(a * PIECE, HALF)
-            nc.vector.quantize_mx(
-                out=dy_codes[h][:, first : first + PIECE].bitcast(E5M2),
-                scales=dy_scales[h][:, first : first + PIECE],
-                in_=dy_bf[a],
-            )
+            cols = slice(a * PIECE, (a + 1) * PIECE)
+            nc.vector.quantize_mx(out=dy_codes[:, cols].bitcast(E5M2), scales=dy_scales[:, cols], in_=dy_bf[a][:])
 
-        bank = {(0, 0): 0, (1, 0): 1, (0, 1): 2, (1, 1): 3, (2, 0): 1, (2, 1): 0, (3, 0): 2, (3, 1): 3}
-        acc = {}
-
-        def product(g, h):
-            acc[g, h] = psum.tile([P, HALF], F32, name="acc%d_%d" % (g, h), tag="bank%d" % bank[g, h])
+        def product(g, j0, j1, bank):
+            acc = psum.tile([P, HALF], F32, name="acc%d_%d" % (g, j0), tag="bank%d" % bank)
             for part in range(2):
                 nc.tensor.matmul_mx(
-                    out=acc[g, h][:],
+                    out=acc[:, : j1 - j0],
                     lhsT=w_codes[g][:, part * P : (part + 1) * P].bitcast(E4M3),
                     lhsT_scale=w_scales[g][:, part * P : (part + 1) * P],
-                    rhs=dy_codes[h][:].bitcast(E5M2),
-                    rhs_scale=dy_scales[h][:],
+                    rhs=dy_codes[:, j0:j1].bitcast(E5M2),
+                    rhs_scale=dy_scales[:, j0:j1],
                     start=part == 0,
                     stop=part == 1,
                 )
+            return acc[:, : j1 - j0]
 
-        def evacuate(g, halves, tag):
-            dx = keep.tile([P, len(halves) * HALF], F32, name="dx%d_%d" % (g, halves[0]), tag=tag, align_bytes=64)
-            for at, h in enumerate(halves):
-                nc.scalar.copy(out=dx[:, at * HALF : (at + 1) * HALF], in_=acc[g, h][:])
-            return dx[:]
+        def own(columns, tag):
+            return keep.tile([P, columns], F32, name=tag, tag=tag, align_bytes=64)[:]
+
+        def sums(g, j0, j1, banks, dx):
+            step = (j1 - j0) // len(banks)
+            for at, bank in enumerate(banks):
+                acc = product(g, j0 + at * step, j0 + (at + 1) * step, bank)
+                nc.scalar.copy(out=dx[:, at * step : (at + 1) * step], in_=acc)
+            return dx
 
         def scatter(g, j0, j1, dx):
             nc.vector.tensor_tensor(
@@ -161,44 +170,41 @@ def tile_list_embg_hl_noneP_kernel(tc, dy, w, wgo, offs, out_0, out_1, out_2):
             page[g] = keep.tile([P, T], F32, name="page%d" % g, tag=tag, align_bytes=64)
             nc.gpsimd.memset(page[g][:], 0.0)
 
-        mask(0)
+        mask(0, 0)
+        mask(0, 1)
         round_hi(0, 0)
         subtract(0, 0)
-        round_dy(0, nc.scalar.copy)
-        subtract(0, 1)
+        round_dy(0)
         quantize_w(0, 1, w_bf[0])
-        round_dy(1, nc.vector.tensor_copy)
         quantize_dy(0)
-        quantize_dy(1)
-        product(0, 0)
-        dx00 = evacuate(0, [0], "dx00")
-        scatter(0, 0, HALF, dx00)
-        round_hi(0, 1)
-        mask(1)
+        dx00 = sums(0, 0, PIECE, [0], own(PIECE, "dx00"))
+        subtract(0, 1)
+        mask(1, 0)
+        mask(1, 1)
         round_hi(1, 0)
         subtract(1, 0)
-        round_hi(1, 1)
-        subtract(1, 1)
         quantize_w(1, 2, w_bf[1])
-        product(1, 0)
-        round_dy(2, nc.scalar.copy)
-        round_dy(3, nc.scalar.copy)
-        nc.vector.quantize_mx(out=dy_codes[1][:].bitcast(E5M2), scales=dy_scales[1][:], in_=late_bf[:, : 2 * width])
-        quantize_w(2, 4, late_bf[:, 2 * width :])
-        product(0, 1)
-        product(1, 1)
-        dx10 = dy_raw[3][:].rearrange("p i c -> p (i c)")[:, :HALF]
-        nc.scalar.copy(out=dx10, in_=acc[1, 0][:])
-        clear_page(2, "late")
-        scatter(1, 0, HALF, dx10)
-        dx01 = evacuate(0, [1], "dx01")
-        dx11 = evacuate(1, [1], "dx11")
-        for g in range(2, PACK):
-            for h in range(J // HALF):
-                product(g, h)
-        dx2 = evacuate(2, [0, 1], "dx2")
-        dx3 = evacuate(3, [0, 1], "dx3")
-        clear_page(3, "dy_raw3")
+        subtract(1, 1)
+        scatter(0, 0, PIECE, dx00)
+        round_dy(1)
+        dx10 = sums(1, 0, PIECE, [1], dy_raw[1][:, :PIECE])
+        quantize_dy(1)
+        scatter(1, 0, PIECE, dx10)
+        round_dy(2)
+        dx01 = sums(0, PIECE, HALF, [2], dy_raw[2][:, :PIECE])
+        quantize_dy(2)
+        scatter(0, PIECE, HALF, dx01)
+        round_dy(3)
+        dx11 = sums(1, PIECE, HALF, [3], dy_raw[3][:, :PIECE])
+        quantize_dy(3)
+        scatter(1, PIECE, HALF, dx11)
+        dx02 = sums(0, HALF, J, [4], own(HALF, "dx02"))
+        dx12 = sums(1, HALF, J, [5], own(HALF, "dx12"))
+        round_hi(0, 1)
+        round_hi(1, 1)
+        quantize_w(2, 4, w_late[:])
+        dx2 = sums(2, 0, J, [6, 7], own(J, "dx2"))
+        dx3 = sums(3, 0, J, [0, 1], own(J, "dx3"))
 
         y_bf = keep.tile([P, T, PACK], BF16, name="y_bf", align_bytes=64)
         runs = T // HALF
@@ -222,9 +228,11 @@ def tile_list_embg_hl_noneP_kernel(tc, dy, w, wgo, offs, out_0, out_1, out_2):
                 in_=back[:].unsqueeze(2).to_broadcast([P, HALF, 2]),
             )
 
-        scatter(0, HALF, J, dx01)
+        scatter(0, HALF, J, dx02)
+        clear_page(2, "dx02")
         turn(0)
-        scatter(1, HALF, J, dx11)
+        scatter(1, HALF, J, dx12)
+        clear_page(3, "dx12")
         turn(1)
         for c in range(runs):
             turn_back(c)

@@ -41,15 +41,24 @@ def tile_list_embg_hl_noneP_kernel(tc, dy, w, wgo, offs, out_0, out_1, out_2):
         out_rows = out_0.rearrange("(p r) t -> p r t", r=PACK)
 
         offsets = keep.tile([P, J // GROUP], U16, name="offsets")
-        w_raw = [keep.tile([P, PACK, PIECE], F32, name="w_raw%d" % a) for a in range(N // PIECE)]
-        dy_raw = [keep.tile([P, PACK * PIECE], F32, name="dy_raw%d" % a, align_bytes=64) for a in range(J // PIECE)]
+        w_raw = [keep.tile([P, PACK * PIECE], F32, name="w_raw%d" % a) for a in range(N // PIECE)]
+        raw = PACK * PIECE
+        first = keep.tile([P, raw + 2 * (HALF - P)], F32, name="first", align_bytes=64)
+        second = keep.tile([P, raw + HALF - P], F32, name="second", align_bytes=64)
+        dy_raw = [first[:, HALF - P : HALF - P + raw], second[:, HALF - P :]] + [
+            keep.tile([P, raw], F32, name="dy_raw%d" % a, align_bytes=64)[:] for a in range(2, J // PIECE)
+        ]
         weight = keep.tile([P, J], F32, name="weight")
 
         def load_w(a):
-            nc.sync.dma_start(out=w_raw[a][:], in_=w_rows[:, :, a * PIECE : (a + 1) * PIECE])
+            for h in range(2):
+                nc.sync.dma_start(
+                    out=w_raw[a][:, h * HALF : (h + 1) * HALF].rearrange("p (i c) -> p i c", i=2),
+                    in_=w_rows[:, 2 * h : 2 * h + 2, a * PIECE : (a + 1) * PIECE],
+                )
 
         def load_dy(a):
-            nc.sync.dma_start(out=dy_raw[a][:].rearrange("p (i c) -> p i c", i=PACK), in_=dy_rows[:, :, a * PIECE : (a + 1) * PIECE])
+            nc.sync.dma_start(out=dy_raw[a].rearrange("p (i c) -> p i c", i=PACK), in_=dy_rows[:, :, a * PIECE : (a + 1) * PIECE])
 
         def load_weight(h):
             nc.sync.dma_start(out=weight[:, h * HALF : (h + 1) * HALF], in_=wgo[:, h * HALF : (h + 1) * HALF])
@@ -75,54 +84,46 @@ def tile_list_embg_hl_noneP_kernel(tc, dy, w, wgo, offs, out_0, out_1, out_2):
 
         width = PIECE * PACK
         dy_bf = [keep.tile([P, width], BF16, name="dy_bf%d" % a, align_bytes=64) for a in range(J // PIECE)]
-        w_first = keep.tile([P, width], BF16, name="w_first", align_bytes=64)
-        w_bf = [w_first[:], dy_raw[0][:, :HALF].bitcast(BF16)]
-        w_late = keep.tile([P, 2 * width], BF16, name="w_late", align_bytes=64)
-        hi_own = [keep.tile([P, HALF], F32, name="hi%d" % a) for a in range(3)]
-        hi_flat = [tile[:] for tile in hi_own] + [dy_raw[0][:, HALF:]]
-        hi = {divmod(at, 2): flat.rearrange("p (i q b) -> p i q b", i=PACK, b=2) for at, flat in enumerate(hi_flat)}
+        w_bf = [keep.tile([P, width], BF16, name="w_bf0", align_bytes=64)[:], first[:, raw + HALF - 2 * P :].bitcast(BF16)]
+        w_late = [first[:, :HALF].bitcast(BF16), second[:, :HALF].bitcast(BF16)]
+        hi = [keep.tile([P, width], F32, name="hi%d" % a)[:] for a in range(N // PIECE)]
 
         def slots(ap, pair):
-            return ap.rearrange("p i (q r) -> p i q r", r=PACK)[:, :, :, 2 * pair : 2 * pair + 2]
+            return ap.rearrange("p (i q r) -> p q i r", i=PACK, r=PACK)[:, :, :, 2 * pair : 2 * pair + 2]
 
         def dealt(a, pair, part):
             if pair == 0:
                 return w_bf[a].rearrange("p (s q b i) -> p s q i b", s=2, b=2, i=PACK)[:, part]
-            both = w_late[:].rearrange("p (b s m i) -> p s m i b", b=2, s=2, i=PACK)
-            return both[:, part, a * WORDS : (a + 1) * WORDS]
+            both = w_late[part].rearrange("p (b m i) -> p m i b", b=2, i=PACK)
+            return both[:, a * WORDS : (a + 1) * WORDS]
 
-        def by_column(ap):
-            return ap.rearrange("p i q b -> p q i b")
-
-        def mask(a, pair):
+        def mask(a, h):
+            rows = slice(h * HALF, (h + 1) * HALF)
             nc.vector.tensor_scalar(
-                out=hi_flat[2 * a + pair].bitcast(I32).rearrange("p (i q b) -> p i q b", i=PACK, b=2),
-                in0=slots(w_raw[a][:].bitcast(I32), pair),
+                out=hi[a][:, rows].bitcast(I32),
+                in0=w_raw[a][:, rows].bitcast(I32),
                 scalar1=HI_MASK,
                 scalar2=None,
                 op0=ALU.bitwise_and,
             )
 
         def round_hi(a, pair):
-            nc.scalar.copy(out=dealt(a, pair, 0), in_=by_column(hi[a, pair]))
+            nc.scalar.copy(out=dealt(a, pair, 1), in_=slots(hi[a], pair))
 
         def subtract(a, pair):
             nc.vector.tensor_tensor(
-                out=dealt(a, pair, 1),
-                in0=by_column(slots(w_raw[a][:], pair)),
-                in1=by_column(hi[a, pair]),
-                op=ALU.subtract,
+                out=dealt(a, pair, 0), in0=slots(w_raw[a][:], pair), in1=slots(hi[a], pair), op=ALU.subtract
             )
 
         w_codes, w_scales = {}, {}
 
-        def quantize_w(g0, g1, values):
-            codes = keep.tile([P, (g1 - g0) * 2 * P], U32, name="w_codes%d" % g0, align_bytes=64)
-            scales = keep.tile([P, (g1 - g0) * 2 * P], U8, name="w_scales%d" % g0, align_bytes=64)
+        def quantize_w(keys, values):
+            name = "%d_%d" % keys[0]
+            codes = keep.tile([P, 2 * P], U32, name="w_codes" + name, align_bytes=64)
+            scales = keep.tile([P, 2 * P], U8, name="w_scales" + name, align_bytes=64)
             nc.vector.quantize_mx(out=codes[:].bitcast(E4M3), scales=scales[:], in_=values)
-            for g in range(g0, g1):
-                cols = slice((g - g0) * 2 * P, (g - g0 + 1) * 2 * P)
-                w_codes[g], w_scales[g] = codes[:, cols], scales[:, cols]
+            for at, key in enumerate(keys):
+                w_codes[key], w_scales[key] = codes[:, at * P : (at + 1) * P], scales[:, at * P : (at + 1) * P]
 
         dy_codes = keep.tile([P, J], U32, name="dy_codes", align_bytes=64)
         dy_scales = keep.tile([P, J], U8, name="dy_scales", align_bytes=64)
@@ -130,7 +131,7 @@ def tile_list_embg_hl_noneP_kernel(tc, dy, w, wgo, offs, out_0, out_1, out_2):
         def round_dy(a):
             nc.scalar.copy(
                 out=dy_bf[a][:].rearrange("p (c e i) -> p c i e", e=4, i=PACK),
-                in_=dy_raw[a][:].rearrange("p (i c e) -> p c i e", e=4, i=PACK),
+                in_=dy_raw[a].rearrange("p (i c e) -> p c i e", e=4, i=PACK),
             )
 
         def quantize_dy(a):
@@ -142,8 +143,8 @@ def tile_list_embg_hl_noneP_kernel(tc, dy, w, wgo, offs, out_0, out_1, out_2):
             for part in range(2):
                 nc.tensor.matmul_mx(
                     out=acc[:, : j1 - j0],
-                    lhsT=w_codes[g][:, part * P : (part + 1) * P].bitcast(E4M3),
-                    lhsT_scale=w_scales[g][:, part * P : (part + 1) * P],
+                    lhsT=w_codes[g, part].bitcast(E4M3),
+                    lhsT_scale=w_scales[g, part],
                     rhs=dy_codes[:, j0:j1].bitcast(E5M2),
                     rhs_scale=dy_scales[:, j0:j1],
                     start=part == 0,
@@ -175,7 +176,7 @@ def tile_list_embg_hl_noneP_kernel(tc, dy, w, wgo, offs, out_0, out_1, out_2):
         round_hi(0, 0)
         subtract(0, 0)
         round_dy(0)
-        quantize_w(0, 1, w_bf[0])
+        quantize_w([(0, 0), (0, 1)], w_bf[0])
         quantize_dy(0)
         dx00 = sums(0, 0, PIECE, [0], own(PIECE, "dx00"))
         subtract(0, 1)
@@ -183,27 +184,28 @@ def tile_list_embg_hl_noneP_kernel(tc, dy, w, wgo, offs, out_0, out_1, out_2):
         mask(1, 1)
         round_hi(1, 0)
         subtract(1, 0)
-        quantize_w(1, 2, w_bf[1])
+        quantize_w([(1, 0), (1, 1)], w_bf[1])
         subtract(1, 1)
         scatter(0, 0, PIECE, dx00)
         round_dy(1)
-        dx10 = sums(1, 0, PIECE, [1], dy_raw[1][:, :PIECE])
+        dx10 = sums(1, 0, PIECE, [1], dy_raw[1][:, PIECE:HALF])
         quantize_dy(1)
+        round_hi(0, 1)
+        round_hi(1, 1)
         scatter(1, 0, PIECE, dx10)
         round_dy(2)
         dx01 = sums(0, PIECE, HALF, [2], dy_raw[2][:, :PIECE])
         quantize_dy(2)
+        for part in range(2):
+            quantize_w([(2, part), (3, part)], w_late[part])
         scatter(0, PIECE, HALF, dx01)
         round_dy(3)
         dx11 = sums(1, PIECE, HALF, [3], dy_raw[3][:, :PIECE])
         quantize_dy(3)
         scatter(1, PIECE, HALF, dx11)
-        dx02 = sums(0, HALF, J, [4], own(HALF, "dx02"))
+        dx02 = sums(0, HALF, J, [4, 6], own(HALF, "dx02"))
         dx12 = sums(1, HALF, J, [5], own(HALF, "dx12"))
-        round_hi(0, 1)
-        round_hi(1, 1)
-        quantize_w(2, 4, w_late[:])
-        dx2 = sums(2, 0, J, [6, 7], own(J, "dx2"))
+        dx2 = sums(2, 0, J, [2, 3], own(J, "dx2"))
         dx3 = sums(3, 0, J, [0, 1], own(J, "dx3"))
 
         y_bf = keep.tile([P, T, PACK], BF16, name="y_bf", align_bytes=64)

@@ -221,14 +221,32 @@ def tile_list_embg_hl_noneP_kernel(tc, dy, w, wgo, offs, out_0, out_1, out_2):
                     nc.tensor.transpose(turned[:, u, :], page[g][:, first : first + P], identity[:])
                 nc.scalar.copy(out=pairs[c][:, :, g * P : (g + 1) * P], in_=turned[:])
 
-        def turn_back(c):
+        def turn_back(c, blocks):
             back = psum.tile([P, HALF], F32, name="back%d" % c, tag="bank%d" % c)
-            for u in range(PACK):
+            for u in range(blocks):
                 nc.tensor.transpose(back[:, u * P : (u + 1) * P], pairs[c][:, u, :].bitcast(F32), identity[:])
             nc.scalar.copy(
-                out=y_bf[:, c * HALF : (c + 1) * HALF, :].bitcast(F32),
-                in_=back[:].unsqueeze(2).to_broadcast([P, HALF, 2]),
+                out=y_bf[:, c * HALF : c * HALF + blocks * P, :].bitcast(F32),
+                in_=back[:, : blocks * P].unsqueeze(2).to_broadcast([P, blocks * P, 2]),
             )
+
+        def turn_rear():
+            turned = psum.tile([P, 2, P], F32, name="turned_rear", tag="bank%d" % (runs - 1))
+            for u in range(2):
+                first = T - CHUNK + u * P
+                nc.tensor.transpose(turned[:, u, :], page[2][:, first : first + P], identity[:])
+            words = dy_bf[3][:, : 2 * CHUNK].rearrange("p (u q e) -> p u q e", u=2, e=2)
+            nc.scalar.copy(out=words[:, :, :, 0], in_=turned[:])
+            return words
+
+        def turn_rear_back(words):
+            back = psum.tile([P, 2, 2, P], F32, name="back_rear", tag="bank%d" % (runs - 2))
+            for u in range(2):
+                nc.tensor.transpose(back[:, 0, u, :], pairs[runs - 1][:, 2 + u, :].bitcast(F32), identity[:])
+                nc.tensor.transpose(
+                    back[:, 1, u, :], words[:, u].rearrange("p q e -> p (q e)").bitcast(F32), identity[:]
+                )
+            nc.scalar.copy(out=y_bf[:, T - CHUNK :, :].bitcast(F32), in_=back[:].rearrange("p w u t -> p (u t) w"))
 
         scatter(0, HALF, J, dx02)
         clear_page(2, "dx02")
@@ -237,11 +255,13 @@ def tile_list_embg_hl_noneP_kernel(tc, dy, w, wgo, offs, out_0, out_1, out_2):
         clear_page(3, "dx12")
         turn(1)
         for c in range(runs):
-            turn_back(c)
+            turn_back(c, PACK if c < runs - 1 else 2)
         scatter(2, 0, J, dx2)
         nc.sync.dma_start(out=out_rows[:, 2, :], in_=page[2][:])
+        rear = turn_rear()
         nc.scalar.copy(out=y_bf[:, :SPLIT, 2:4], in_=page[2][:, :SPLIT].unsqueeze(2).to_broadcast([P, SPLIT, 2]))
-        nc.scalar.copy(out=y_bf[:, SPLIT:, 2], in_=page[2][:, SPLIT:])
+        turn_rear_back(rear)
+        nc.scalar.copy(out=y_bf[:, SPLIT : T - CHUNK, 2], in_=page[2][:, SPLIT : T - CHUNK])
         scatter(3, 0, J, dx3)
         nc.sync.dma_start(out=out_rows[:, 3, :], in_=page[3][:])
 

@@ -26,7 +26,8 @@ HI_MASK = -(1 << 20)
 CHUNK = 256
 CHUNKS = T // CHUNK
 VECTOR_CHUNKS = CHUNKS // 2
-SPLIT = VECTOR_CHUNKS * CHUNK
+SPLIT = VECTOR_CHUNKS * CHUNK - P
+FILL = P
 QUADRANTS = 4
 
 
@@ -259,19 +260,21 @@ def tile_list_embg_hl_noneP_kernel(tc, dy, w, wgo, offs, out_0, out_1, out_2):
         scatter(2, 0, J, dx2)
         nc.sync.dma_start(out=out_rows[:, 2, :], in_=page[2][:])
         rear = turn_rear()
-        nc.scalar.copy(out=y_bf[:, :SPLIT, 2:4], in_=page[2][:, :SPLIT].unsqueeze(2).to_broadcast([P, SPLIT, 2]))
+        nc.scalar.copy(
+            out=y_bf[:, FILL:SPLIT, 2:4], in_=page[2][:, FILL:SPLIT].unsqueeze(2).to_broadcast([P, SPLIT - FILL, 2])
+        )
         turn_rear_back(rear)
         nc.scalar.copy(out=y_bf[:, SPLIT : T - CHUNK, 2], in_=page[2][:, SPLIT : T - CHUNK])
         scatter(3, 0, J, dx3)
         nc.sync.dma_start(out=out_rows[:, 3, :], in_=page[3][:])
+        nc.vector.tensor_copy(out=y_bf[:, :FILL, 2], in_=page[2][:, :FILL])
 
         y_codes = keep.tile([P, T], U32, name="y_codes", align_bytes=64)
         y_scales = keep.tile([P, 2 * CHUNK], U8, name="y_scales", align_bytes=64)
         words = out_1[0].rearrange("p t i -> p (t i)").bitcast(I32)
 
-        def round_last_page(c, copy):
-            cols = slice(c * CHUNK, (c + 1) * CHUNK)
-            copy(out=y_bf[:, cols, 3], in_=page[3][:, cols])
+        def round_last_page(t0, t1, copy):
+            copy(out=y_bf[:, t0:t1, 3], in_=page[3][:, t0:t1])
 
         def quantize_y(c):
             cols = slice(c * CHUNK, (c + 1) * CHUNK)
@@ -285,12 +288,13 @@ def tile_list_embg_hl_noneP_kernel(tc, dy, w, wgo, offs, out_0, out_1, out_2):
             cols = slice(c0 * CHUNK, c1 * CHUNK)
             nc.sync.dma_start(out=words[:, cols], in_=y_codes[:, cols].bitcast(I32))
 
+        round_last_page(SPLIT, VECTOR_CHUNKS * CHUNK, nc.scalar.copy)
         for c in range(VECTOR_CHUNKS, CHUNKS):
-            round_last_page(c, nc.scalar.copy)
-        round_last_page(0, nc.vector.tensor_copy)
+            round_last_page(c * CHUNK, (c + 1) * CHUNK, nc.scalar.copy)
+        round_last_page(0, CHUNK, nc.vector.tensor_copy)
         for c in range(CHUNKS):
             if c + 1 < VECTOR_CHUNKS:
-                round_last_page(c + 1, nc.vector.tensor_copy)
+                round_last_page((c + 1) * CHUNK, min((c + 2) * CHUNK, SPLIT), nc.vector.tensor_copy)
             quantize_y(c)
             if c >= CHUNKS - 2:
                 store_words(c, c + 1)

from contextlib import ExitStack

import concourse.mybir as mybir
from concourse.masks import make_identity

K, N, T, J = 512, 512, 2048, 1024
FLOPS = 2 * 2 * K * N * J

F32 = mybir.dt.float32
BF16 = mybir.dt.bfloat16
I32 = mybir.dt.int32
U32 = mybir.dt.uint32
U16 = mybir.dt.uint16
U8 = mybir.dt.uint8
E4M3 = mybir.dt.float8_e4m3fn_x4
E5M2 = mybir.dt.float8_e5m2_x4
ALU = mybir.AluOpType

P = 128
PACK = 4
GROUP = 16
HALF = 512
PIECE = 256
WORDS = PIECE // PACK
HI_MASK = -(1 << 20)
CHUNK = 256
CHUNKS = T // CHUNK
VECTOR_CHUNKS = CHUNKS // 2
SPLIT = VECTOR_CHUNKS * CHUNK - P
FILL = P
QUADRANTS = 4


def tile_list_embg_hl_noneP_kernel(tc, dy, w, wgo, offs, out_0, out_1, out_2):
    nc = tc.nc
    with ExitStack() as ctx:
        keep = ctx.enter_context(tc.tile_pool(name="keep", bufs=1))
        psum = ctx.enter_context(tc.psum_pool(name="psum", bufs=1))

        w_rows = w.rearrange("(p i) n -> p i n", i=PACK)
        dy_rows = dy.rearrange("(p i) j -> p i j", i=PACK)
        out_rows = out_0.rearrange("(p r) t -> p r t", r=PACK)

        offsets = keep.tile([P, J // GROUP], U16, name="offsets")
        w_raw = [keep.tile([P, PACK * PIECE], F32, name="w_raw%d" % a) for a in range(N // PIECE)]
        raw = PACK * PIECE
        first = keep.tile([P, raw + 2 * (HALF - P)], F32, name="first", align_bytes=64)
        second = keep.tile([P, raw + HALF - P], F32, name="second", align_bytes=64)
        dy_raw = [first[:, HALF - P : HALF - P + raw], second[:, HALF - P :]] + [
            keep.tile([P, raw], F32, name="dy_raw%d" % a, align_bytes=64)[:] for a in range(2, J // PIECE)
        ]
        weight = keep.tile([P, J], F32, name="weight")

        def load_w(a):
            for h in range(2):
                nc.sync.dma_start(
                    out=w_raw[a][:, h * HALF : (h + 1) * HALF].rearrange("p (i c) -> p i c", i=2),
                    in_=w_rows[:, 2 * h : 2 * h + 2, a * PIECE : (a + 1) * PIECE],
                )

        def load_dy(a):
            nc.sync.dma_start(out=dy_raw[a].rearrange("p (i c) -> p i c", i=PACK), in_=dy_rows[:, :, a * PIECE : (a + 1) * PIECE])

        def load_weight(h):
            nc.sync.dma_start(out=weight[:, h * HALF : (h + 1) * HALF], in_=wgo[:, h * HALF : (h + 1) * HALF])

        load_w(0)
        load_dy(0)
        load_w(1)
        nc.sync.dma_start(offsets[:], offs)
        load_weight(0)
        load_dy(1)
        load_dy(2)
        load_dy(3)
        load_weight(1)

        page = {}
        page[0] = keep.tile([P, T], F32, name="page0")
        nc.vector.memset(page[0][:, : T - 1], 0.0)
        nc.vector.memset(page[0][:, T - 1 :], 0.0)
        identity = keep.tile([P, P], F32, name="identity")
        make_identity(nc, identity[:])
        page[1] = keep.tile([P, T], F32, name="page1")
        nc.gpsimd.memset(page[1][:], 0.0)

        width = PIECE * PACK
        dy_bf = [keep.tile([P, width], BF16, name="dy_bf%d" % a, align_bytes=64) for a in range(J // PIECE)]
        w_bf = [keep.tile([P, width], BF16, name="w_bf0", align_bytes=64)[:], first[:, raw + HALF - 2 * P :].bitcast(BF16)]
        w_late = [first[:, :HALF].bitcast(BF16), second[:, :HALF].bitcast(BF16)]
        hi = [keep.tile([P, width], F32, name="hi%d" % a)[:] for a in range(N // PIECE)]

        def slots(ap, pair):
            return ap.rearrange("p (i q r) -> p q i r", i=PACK, r=PACK)[:, :, :, 2 * pair : 2 * pair + 2]

        def dealt(a, pair, part):
            if pair == 0:
                return w_bf[a].rearrange("p (s q b i) -> p s q i b", s=2, b=2, i=PACK)[:, part]
            both = w_late[part].rearrange("p (b m i) -> p m i b", b=2, i=PACK)
            return both[:, a * WORDS : (a + 1) * WORDS]

        def mask(a, h):
            rows = slice(h * HALF, (h + 1) * HALF)
            nc.vector.tensor_scalar(
                out=hi[a][:, rows].bitcast(I32),
                in0=w_raw[a][:, rows].bitcast(I32),
                scalar1=HI_MASK,
                scalar2=None,
                op0=ALU.bitwise_and,
            )

        def round_hi(a, pair):
            nc.scalar.copy(out=dealt(a, pair, 1), in_=slots(hi[a], pair))

        def subtract(a, pair):
            nc.vector.tensor_tensor(
                out=dealt(a, pair, 0), in0=slots(w_raw[a][:], pair), in1=slots(hi[a], pair), op=ALU.subtract
            )

        w_codes, w_scales = {}, {}

        def quantize_w(keys, values):
            name = "%d_%d" % keys[0]
            codes = keep.tile([P, 2 * P], U32, name="w_codes" + name, align_bytes=64)
            scales = keep.tile([P, 2 * P], U8, name="w_scales" + name, align_bytes=64)
            nc.vector.quantize_mx(out=codes[:].bitcast(E4M3), scales=scales[:], in_=values)
            for at, key in enumerate(keys):
                w_codes[key], w_scales[key] = codes[:, at * P : (at + 1) * P], scales[:, at * P : (at + 1) * P]

        dy_codes = keep.tile([P, J], U32, name="dy_codes", align_bytes=64)
        dy_scales = keep.tile([P, J], U8, name="dy_scales", align_bytes=64)

        def round_dy(a):
            nc.scalar.copy(
                out=dy_bf[a][:].rearrange("p (c e i) -> p c i e", e=4, i=PACK),
                in_=dy_raw[a].rearrange("p (i c e) -> p c i e", e=4, i=PACK),
            )

        def quantize_dy(a):
            cols = slice(a * PIECE, (a + 1) * PIECE)
            nc.vector.quantize_mx(out=dy_codes[:, cols].bitcast(E5M2), scales=dy_scales[:, cols], in_=dy_bf[a][:])

        def product(g, j0, j1, bank):
            acc = psum.tile([P, HALF], F32, name="acc%d_%d" % (g, j0), tag="bank%d" % bank)
            for part in range(2):
                nc.tensor.matmul_mx(
                    out=acc[:, : j1 - j0],
                    lhsT=w_codes[g, part].bitcast(E4M3),
                    lhsT_scale=w_scales[g, part],
                    rhs=dy_codes[:, j0:j1].bitcast(E5M2),
                    rhs_scale=dy_scales[:, j0:j1],
                    start=part == 0,
                    stop=part == 1,
                )
            return acc[:, : j1 - j0]

        def own(columns, tag):
            return keep.tile([P, columns], F32, name=tag, tag=tag, align_bytes=64)[:]

        def sums(g, j0, j1, banks, dx):
            step = (j1 - j0) // len(banks)
            for at, bank in enumerate(banks):
                acc = product(g, j0 + at * step, j0 + (at + 1) * step, bank)
                nc.scalar.copy(out=dx[:, at * step : (at + 1) * step], in_=acc)
            return dx

        def scatter(g, j0, j1, dx):
            nc.vector.tensor_tensor(
                page[g][:].indirect(offsets[:, j0 // GROUP : j1 // GROUP]), dx, weight[:, j0:j1], ALU.mult
            )

        def clear_page(g, tag):
            page[g] = keep.tile([P, T], F32, name="page%d" % g, tag=tag, align_bytes=64)
            nc.gpsimd.memset(page[g][:], 0.0)

        mask(0, 0)
        mask(0, 1)
        round_hi(0, 0)
        subtract(0, 0)
        round_dy(0)
        quantize_w([(0, 0), (0, 1)], w_bf[0])
        quantize_dy(0)
        dx00 = sums(0, 0, PIECE, [0], own(PIECE, "dx00"))
        subtract(0, 1)
        mask(1, 0)
        mask(1, 1)
        round_hi(1, 0)
        subtract(1, 0)
        quantize_w([(1, 0), (1, 1)], w_bf[1])
        subtract(1, 1)
        scatter(0, 0, PIECE, dx00)
        round_dy(1)
        dx10 = sums(1, 0, PIECE, [1], dy_raw[1][:, PIECE:HALF])
        quantize_dy(1)
        round_hi(0, 1)
        round_hi(1, 1)
        scatter(1, 0, PIECE, dx10)
        round_dy(2)
        dx01 = sums(0, PIECE, HALF, [2], dy_raw[2][:, :PIECE])
        quantize_dy(2)
        for part in range(2):
            quantize_w([(2, part), (3, part)], w_late[part])
        scatter(0, PIECE, HALF, dx01)
        round_dy(3)
        dx11 = sums(1, PIECE, HALF, [3], dy_raw[3][:, :PIECE])
        quantize_dy(3)
        scatter(1, PIECE, HALF, dx11)
        dx02 = sums(0, HALF, J, [4, 6], own(HALF, "dx02"))
        dx12 = sums(1, HALF, J, [5], own(HALF, "dx12"))
        dx2 = sums(2, 0, J, [2, 3], own(J, "dx2"))
        dx3 = sums(3, 0, J, [0, 1], own(J, "dx3"))

        y_bf = keep.tile([P, T, PACK], BF16, name="y_bf", align_bytes=64)
        runs = T // HALF
        pairs = [keep.tile([P, PACK, 2 * P], BF16, name="pairs%d" % c, align_bytes=64) for c in range(runs)]

        def turn(g):
            nc.sync.dma_start(out=out_rows[g * WORDS : (g + 1) * WORDS, 0:2, :], in_=page[g][:])
            for c in range(runs):
                turned = psum.tile([P, PACK, P], F32, name="turned%d_%d" % (g, c), tag="bank%d" % c)
                for u in range(PACK):
                    first = c * HALF + u * P
                    nc.tensor.transpose(turned[:, u, :], page[g][:, first : first + P], identity[:])
                nc.scalar.copy(out=pairs[c][:, :, g * P : (g + 1) * P], in_=turned[:])

        def turn_back(c, blocks):
            back = psum.tile([P, HALF], F32, name="back%d" % c, tag="bank%d" % c)
            for u in range(blocks):
                nc.tensor.transpose(back[:, u * P : (u + 1) * P], pairs[c][:, u, :].bitcast(F32), identity[:])
            nc.scalar.copy(
                out=y_bf[:, c * HALF : c * HALF + blocks * P, :].bitcast(F32),
                in_=back[:, : blocks * P].unsqueeze(2).to_broadcast([P, blocks * P, 2]),
            )

        def turn_rear():
            turned = psum.tile([P, 2, P], F32, name="turned_rear", tag="bank%d" % (runs - 1))
            for u in range(2):
                first = T - CHUNK + u * P
                nc.tensor.transpose(turned[:, u, :], page[2][:, first : first + P], identity[:])
            words = dy_bf[3][:, : 2 * CHUNK].rearrange("p (u q e) -> p u q e", u=2, e=2)
            nc.scalar.copy(out=words[:, :, :, 0], in_=turned[:])
            return words

        def turn_rear_back(words):
            back = psum.tile([P, 2, 2, P], F32, name="back_rear", tag="bank%d" % (runs - 2))
            for u in range(2):
                nc.tensor.transpose(back[:, 0, u, :], pairs[runs - 1][:, 2 + u, :].bitcast(F32), identity[:])
                nc.tensor.transpose(
                    back[:, 1, u, :], words[:, u].rearrange("p q e -> p (q e)").bitcast(F32), identity[:]
                )
            nc.scalar.copy(out=y_bf[:, T - CHUNK :, :].bitcast(F32), in_=back[:].rearrange("p w u t -> p (u t) w"))

        scatter(0, HALF, J, dx02)
        clear_page(2, "dx02")
        turn(0)
        scatter(1, HALF, J, dx12)
        clear_page(3, "dx12")
        turn(1)
        for c in range(runs):
            turn_back(c, PACK if c < runs - 1 else 2)
        scatter(2, 0, J, dx2)
        nc.sync.dma_start(out=out_rows[:, 2, :], in_=page[2][:])
        rear = turn_rear()
        nc.scalar.copy(
            out=y_bf[:, FILL:SPLIT, 2:4], in_=page[2][:, FILL:SPLIT].unsqueeze(2).to_broadcast([P, SPLIT - FILL, 2])
        )
        turn_rear_back(rear)
        nc.scalar.copy(out=y_bf[:, SPLIT : T - CHUNK, 2], in_=page[2][:, SPLIT : T - CHUNK])
        scatter(3, 0, J, dx3)
        nc.sync.dma_start(out=out_rows[:, 3, :], in_=page[3][:])
        nc.vector.tensor_copy(out=y_bf[:, :FILL, 2], in_=page[2][:, :FILL])

        y_codes = keep.tile([P, T], U32, name="y_codes", align_bytes=64)
        y_scales = keep.tile([P, 2 * CHUNK], U8, name="y_scales", align_bytes=64)
        words = out_1[0].rearrange("p t i -> p (t i)").bitcast(I32)

        def round_last_page(t0, t1, copy):
            copy(out=y_bf[:, t0:t1, 3], in_=page[3][:, t0:t1])

        def quantize_y(c):
            cols = slice(c * CHUNK, (c + 1) * CHUNK)
            nc.vector.quantize_mx(
                out=y_codes[:, cols].bitcast(E4M3),
                scales=y_scales[4 * (c // 2) :, (c % 2) * CHUNK : (c % 2 + 1) * CHUNK],
                in_=y_bf[:, cols, :].rearrange("p t i -> p (t i)"),
            )

        def store_words(c0, c1):
            cols = slice(c0 * CHUNK, c1 * CHUNK)
            nc.sync.dma_start(out=words[:, cols], in_=y_codes[:, cols].bitcast(I32))

        round_last_page(SPLIT, VECTOR_CHUNKS * CHUNK, nc.scalar.copy)
        for c in range(VECTOR_CHUNKS, CHUNKS):
            round_last_page(c * CHUNK, (c + 1) * CHUNK, nc.scalar.copy)
        round_last_page(0, CHUNK, nc.vector.tensor_copy)
        for c in range(CHUNKS):
            if c + 1 < VECTOR_CHUNKS:
                round_last_page((c + 1) * CHUNK, min((c + 2) * CHUNK, SPLIT), nc.vector.tensor_copy)
            quantize_y(c)
            if c >= CHUNKS - 2:
                store_words(c, c + 1)
            elif c % 2:
                store_words(c - 1, c + 1)

        for q in range(QUADRANTS):
            queue = nc.sync if q % 2 else nc.scalar
            queue.dma_start(
                out=out_2[0, 4 * q : 4 * q + 4, :].bitcast(I32).rearrange("s (g x) -> g s x", g=CHUNKS // 2),
                in_=y_scales[32 * q : 32 * q + 16, :].bitcast(I32),
            )
